import numpy as np, ml_dtypes
CORES = [16,18,20,22]
N = 4
import mx_ref
BF = ml_dtypes.bfloat16
def gentries(a):
    return np.ascontiguousarray(a.reshape(8, 16, -1).transpose(0, 2, 1)).reshape(8, -1)
def gtable(e):
    e = np.asarray(e); return np.ascontiguousarray(e.reshape(8, -1, 16).transpose(0, 2, 1)).reshape(128, -1).astype(np.int32)
def gcols(t, e):
    v = np.concatenate([t.reshape(8, 16, -1, 4), np.zeros((8, 16, 1, 4), BF)], axis=2)
    return np.ascontiguousarray(np.stack([v[g][:, e[g]] for g in range(8)])).reshape(128, -1)
def tile(rs):
    return np.stack(rs, axis=2).reshape(128, -1).astype(BF)
def pick(q, e):
    c = np.concatenate([q[0].reshape(128, -1, 4), np.zeros((128, 1, 4), np.uint8)], axis=1); s = np.concatenate([q[1], np.ones((16, 1), np.uint8)], axis=1)
    return (np.ascontiguousarray(c[:, e].reshape(128, -1)), np.ascontiguousarray(s[:, e]))
def join(*qs):
    return (np.concatenate([q[0] for q in qs], axis=1), np.concatenate([q[1] for q in qs], axis=1))
def put(q, e, v):
    c, s = q[0].reshape(128, -1, 4).copy(), q[1].copy(); c[:, e] = v[0].reshape(128, -1, 4); s[:, e] = v[1]
    return (c.reshape(128, -1), s)
def pk(c, s):
    return (np.ascontiguousarray(c), mx_ref.live(s))
def emit(q):
    return q[0], q[1]
def packed(v, rng):
    q = [mx_ref.quantize(np.ascontiguousarray(v[r])) for r in range(N)]
    return np.stack([a for a, b in q]), np.stack([mx_ref.plane(b, rng) for a, b in q])
def values_of_codes():
    e, c = np.zeros((128, 128, 4), np.float32), np.zeros((128, 2, 4), np.uint8)
    e[np.arange(128), np.arange(128), 0] = 1
    c[:127, :, 0] = np.arange(256).reshape(2, 128).T[:127]
    return mx_ref.matmul(mx_ref.quantize(e.reshape(128, 512).astype(BF)), (c.reshape(128, 8), np.full((16, 2), 127, np.uint8))).T.reshape(-1).astype(np.float64)
CODE_VALUE, SCALE_VALUE = values_of_codes(), 2.0 ** (np.arange(256) - 127.0)
def decode(q):
    return (CODE_VALUE[q[0]].reshape(16, 8, -1, 4) * SCALE_VALUE[q[1]][:, None, :, None] + 0.0).reshape(128, -1).astype(np.float32)
def f(rng, *shape):
    return mx_ref.flush((rng.standard_normal(shape, dtype=np.float32) * np.exp2(rng.integers(-2, 3, shape[:-1] + (1,)))).astype(BF))
def wide(rng, *shape, cols=0):
    v = rng.standard_normal(shape, dtype=np.float32) * np.exp2(rng.integers(-12, 13, shape)).astype(np.float32)
    if cols: v *= np.repeat(np.exp2(rng.integers(-cols, cols + 1, shape[:-2] + (1, shape[-1] // 4))) * (rng.random(shape[:-2] + (1, shape[-1] // 4)) > 0.0625), 4, axis=-1).astype(np.float32)
    return mx_ref.flush(v.astype(BF))
C, K, R, H = 320, 128, 3, 6
ROWS_USED = [(16 * g, 16 * g, 8) for g in range(8)] + [(16 * g + 1, 16 * g, 9) for g in range(8)] + [(8, 0, 10)]
def big(v):
    v = np.clip(v.astype(np.float32), -2.0 ** 21, 2.0 ** 21)
    v[np.abs(v) < np.float32(2.0 ** -16)] = 0
    return v.astype(BF)
def numbers_of(rng):
    return {"x": big(f(rng, N, 128, 4 * C)), "u": np.array(f(rng, N, 128, 512)), "v": np.array(f(rng, N, 128, 512))}
def links(rng):
    return np.stack([gtable(rng.integers(0, C, (8, C))) for r in range(N)])
def layers(rng):
    w = np.clip(big(f(rng, N, 128, 2048)).astype(np.float32) * np.float32(0.25), -1.0, 1.0)
    return w.astype(BF).reshape(N, 8, 16, 4, 8, 16, 4)
def weights(rng, w, still=[]):
    for i in still:
        w[:, :, i] = 0
        w[:, :, :, :, :, i] = 0
    c, p = packed(np.ascontiguousarray(w).reshape(N, 128, 2048), rng)
    return {"wc": c, "ws": p}
def setup_inputs(rng):
    return {**numbers_of(rng), "ol": links(rng), **weights(rng, layers(rng))}
def setup_inputs_ties(rng):
    d = numbers_of(rng)
    o = rng.permutation(N)
    x = d["x"].reshape(N, 8, 16, C, 4)
    x[:, :, :3] = 0
    x[:, :, :3, :, 0] = rng.integers(0, 3, (N, 8, 3, C)).astype(np.float32).astype(BF)
    k = np.ones(N, np.float32)
    k[o[0]] = 0
    k[o[1]] = -1
    u = d["u"].reshape(N, 128, 128, 4)
    for i, h, j in ROWS_USED:
        u[:, :, i] = 0
        u[:, h + j - 8, i, 0] = k.astype(BF)
    p = links(rng)
    e = np.stack([rng.permutation(C) for g in range(8)]).reshape(8, -1, 4)
    n = np.zeros((8, C), np.int64)
    np.put_along_axis(n, e.reshape(8, C), np.roll(e, -1, axis=2).reshape(8, C), axis=1)
    p[o[0]] = gtable(n)
    return {"x": x.reshape(N, 128, 4 * C), "u": u.reshape(N, 128, 512), "v": d["v"], "ol": p, **weights(rng, layers(rng), [0, 1, 2])}
def setup_inputs_near(rng):
    d = numbers_of(rng)
    o = rng.permutation(N) % 3
    x = d["x"].astype(np.float32).reshape(N, 8, 16, C, 4)
    x[:, :, 0] = 0
    x[:, :, 8:] = 0
    x[:, :, 0, :, 0] = rng.integers(0, 2, (N, 8, C)) * 2.0 - 1.0
    s = rng.integers(0, 16, (N, 8, 3, C))
    x[:, :, 8:11] = ((s[..., None] >> np.arange(4)) & 1) * np.exp2(np.arange(4) - 23.0)
    x[:, :, 11, :, 0] = 2.0 ** -10
    for r in range(N):
        for g in rng.permutation(8)[:4]: x[r, g, 0, rng.integers(C), 0] = 2.0 ** 20 * rng.choice([-1.0, 1.0])
    u = d["u"].reshape(N, 128, 128, 4)
    for i, h, j in ROWS_USED:
        u[:, :, i] = 0
        for r in range(N):
            k = 1.0 if o[r] == 0 else 2.0 ** -30
            u[r, h + j, i] = k
            if o[r] < 2:
                u[r, h, i, 0] = k
                u[r, h + 11, i, 0] = k
    return {"x": x.reshape(N, 128, 4 * C).astype(BF), "u": u.reshape(N, 128, 512), "v": d["v"], "ol": links(rng), **weights(rng, layers(rng), [0, 8, 9, 10, 11, 12, 13, 14, 15])}
def setup_inputs_chains(rng):
    d = numbers_of(rng)
    o = rng.permutation(N)
    p = []
    for r in range(N):
        e = np.zeros((8, C), np.int64)
        if o[r] == 0:
            n = rng.permutation(C)
            hub = np.sort(n[K - 1:])
            e[:, hub] = hub
            e[:, n[:K - 1]] = hub[rng.permutation(8 * (K - 1)) % (C - K + 1)].reshape(8, K - 1)
        elif o[r] % 2 == 0:
            for g in range(8):
                n = rng.permutation(C)
                e[g, n] = np.roll(n, -1)
        else:
            n = rng.permutation(C)
            low, hub, m = n[:K].reshape(-1, 8), n[K:], np.arange(K // 8)
            e[:, hub] = hub
            g = int(rng.integers(8))
            e[np.ix_([i for i in range(8) if i != g], n[:K])] = hub[rng.permutation(7 * K) % (C - K)].reshape(7, K)
            e[g, low[:, :7]] = low[:, 1:]
            e[g, low[:, 7]] = hub[:K // 8]
            e[g, hub[-(K // 8):]] = low[m, 7 - m % 8]
        p.append(gtable(e))
    x = d["x"].astype(np.float32).reshape(N, 8, 16, C, 4)
    k = rng.random((N, 1, 1, C, 1)) < 0.5
    k[:, :, :, 0] = True
    s = (1.125 + 0.25 * rng.integers(0, 4, x.shape)) * np.exp2(-rng.integers(8, 15, x.shape).astype(np.float64)) * rng.choice([-1.0, 1.0], x.shape)
    s[:, :, ::8, :, 0] = 1.96875 * rng.choice([-1.0, 1.0], (N, 8, 2, C))
    x = np.where(k, s, x).astype(np.float32).astype(BF)
    return {"x": x.reshape(N, 128, 4 * C), "u": d["u"], "v": d["v"], "ol": np.stack(p), **weights(rng, layers(rng))}
def setup_inputs_ends(rng):
    o = rng.permutation(N) % 4
    h = rng.permutation(8)
    a = np.full((N, 8, 16, C, 4), 2.0 ** 21)
    a[:, h[:4]] *= 1 - 0.1 * rng.random((N, 4, 16, C, 4))
    c = rng.integers(0, 2, (N, 1, 1, C, 1)) * 2.0 - 1.0
    c[o == 0] = 1
    c[o == 1] = -1
    a = a * c
    a[o == 3] = 2.0 ** -24
    u = np.full((N, 128, 128, 4), 2.0 ** 30)
    u[o == 3] = 2.0 ** -30
    for g in h[4:]: u[:, np.arange(128) // 16 != g, 16 * g:16 * g + 2] = 0
    k = rng.integers(0, 2, (N, 1, 128, 1)) * 2.0 - 1.0
    k[:, :, 1::16] = 1
    u = u * k + 0.0
    v = rng.choice([-1.0, 1.0], (N, 128, 512)) * np.where(o % 2 == 0, 2.0 ** 30, 2.0 ** -30)[:, None, None]
    w = np.ones((N, 128, 2048), np.float32)
    t = np.zeros((N, 8, C), np.int64)
    for r in range(N):
        if o[r] == 0: t[r] = C - 1
        if o[r] == 2:
            t[r] = np.arange(C)
            w[r] = rng.choice([-1.0, 1.0], (128, 2048))
        if o[r] == 3: t[r] = rng.integers(0, 2, (8, C)) * (C - 1)
    x, u, v = [b.astype(np.float32).astype(BF) for b in (a.reshape(N, 128, 4 * C), u.reshape(N, 128, 512), v)]
    return {"x": x, "u": u, "v": v, "ol": np.stack([gtable(t[r]) for r in range(N)]), **weights(rng, w.astype(BF))}
def setup_inputs_spread(rng):
    d = setup_inputs(rng)
    d["x"] = big(wide(rng, N, 128, 4 * C, cols=6))
    return d
def check_inputs(d):
    b = []
    for k, lo, hi in (("x", -24, 21), ("u", -30, 30), ("v", -30, 30)):
        a = np.abs(d[k].astype(np.float32))
        if not (np.isfinite(a).all() and ((a == 0) | (a >= 2.0 ** lo) & (a <= 2.0 ** hi)).all()): b.append("a value of " + k)
    if not ((d["ol"] >= 0) & (d["ol"] < C)).all(): b.append("an entry of ol")
    none, least, most = [emit(mx_ref.quantize(np.full((128, 16), k, np.float32).astype(BF)))[1][0, 0] for k in (0.0, 2.0 ** -30, 1.0)]
    for r in range(N):
        if ((d["wc"][r] == 0x7F) | (d["wc"][r] == 0xFF)).any(): b.append("wc: a code that is no number")
        s = mx_ref.live(d["ws"][r])
        if ((s != none) & ((s < least) | (s > most))).any(): b.append("ws: a scale out of range")
        elif not (np.abs(decode(pk(d["wc"][r], d["ws"][r]))) <= 1).all(): b.append("W: a number beyond 1")
    return b
def places(s):
    return np.argsort(np.argsort(s, axis=-1, kind="stable"), axis=-1, kind="stable")
def reference(x, u, v, ol, wc, ws):
    qu = [mx_ref.quantize(u[r]) for r in range(N)]
    lay = [pk(wc[r], ws[r]) for r in range(N)]
    now = [x[r] for r in range(N)]
    link = [gentries(ol[r]).astype(np.int64) for r in range(N)]
    for t in range(R):
        means, sent, given, freed, spliced = [], [], [], [], []
        for r in range(N):
            q = mx_ref.quantize(now[r])
            s = mx_ref.matmul(qu[r], q) + np.float32(0.0)
            own = decode(q)
            birth, snap = places(s[8]), places(s[::16])
            hops = [link[r]]
            for i in range(H - 1): hops.append(np.take_along_axis(link[r], hops[-1], axis=1))
            read = hops[-1]
            for p in hops[::-1]: read = np.where(birth[p] <= snap, p, read)
            z = ((own + gcols(own.astype(BF), read).astype(np.float32)) * np.float32(0.5)).astype(BF)
            e = np.argsort(-s[1::16], axis=1, kind="stable")[:, :K]
            count = np.bincount(read.reshape(-1), minlength=C)
            d = np.sort(np.argsort(count, kind="stable")[:K])
            gone = np.zeros(C, bool)
            gone[d] = True
            l = np.tile(np.arange(C), (8, 1))
            for p in hops[::-1]: l = np.where(gone[p], l, p)
            means.append(z)
            sent.append(mx_ref.quantize(gcols(z, e)))
            given.append(e)
            freed.append(d)
            spliced.append(l)
        for r in range(N):
            b4 = (r + N - 1) % N
            a = sent[b4]
            da = decode(a)
            m = tile([mx_ref.matmul(pick(lay[r], np.arange(128 * b, 128 * b + 128)), a) * np.float32(0.0078125) + da[:, b::4] for b in range(4)])
            z = means[r].reshape(128, C, 4).copy()
            z[:, freed[r]] = m.reshape(128, K, 4)
            now[r] = z.reshape(128, 4 * C)
            link[r] = spliced[r]
            link[r][:, freed[r]] = given[b4]
    y, lk = np.zeros((N, 128, C), np.float32), np.zeros((N, 8, C), np.float32)
    oc, osc = np.zeros((N, 128, 4 * C), np.uint8), np.zeros((N, 16, C), np.uint8)
    for r in range(N):
        q = mx_ref.quantize(now[r])
        y[r] = mx_ref.matmul(mx_ref.quantize(v[r]), q)
        lk[r] = link[r]
        oc[r], osc[r] = emit(q)
    return {"y": y, "lk": lk, "oc": oc, "osc": osc}

@@ -1,0 +1,556 @@
+from concourse.mybir import dt, AluOpType, AxisListType, ActivationFunctionType
+
+C, K, R, H = 320, 128, 3, 6
+BIG = 1.0e29
+FAR = 1.0e6
+NSEM = 24
+NT = [max(128, 64 * (m + 1)) for m in range(5)]
+KEYS = ["KE0", "KE1", "KE2", "KE3", "KH0", "KH1", "KH2", "KH3", "Ge", "Go", "SDe", "SDo", "ODe", "ODo", "KB"]
+USEG = ["UB", "US", "USe", "USo", "UO", "UOe", "UOo"]
+EARLY = 10
+ACT_ORDER = (1, 2, 3, 4, 5)
+GATHER_AT = 3
+VEC_COUNTS = 1
+
+APART = ["TB", "eq", "rss", "rso", "hc", "hd", "thx", "e4", "pk", "h4", "kg0", "kg1"] + ["TS%d" % _m for _m in range(5)] + ["TO%d" % _m for _m in range(5)] + ["ps%d" % _m for _m in range(8)]
+
+F8 = "float8_e4m3fn_x4"
+ARENA = {
+    "fc": ("float32", [("pf", 16), ("iof", 320), ("ci", 320), ("cg", 256), ("ms", 320), ("mo", 320), ("m1", 320), ("inm", 16), ("b16", 20), ("one", 32)]),
+    "ic": ("int32", [("pii", 8), ("uli", 56), ("eli", 20), ("ioi", 320)]),
+    "uc": ("uint16", [("ul", 56), ("el", 20)]),
+    "bc": ("bfloat16", [("zb", 1280), ("bm", 320), ("pk", 3200), ("gmk", 384)]),
+    "fp": ("float32", [("sl", 20), ("nsl", 20), ("slo", 20), ("df0", 320), ("df1", 320), ("rss", 20), ("rso", 20)]),
+    "fl": ("float32", [("va", 320), ("inj", 1920), ("aw0", 320), ("aw1", 320), ("a6f", 320), ("dw", 320), ("dx", 320), ("dy", 320), ("y5", 20), ("hs0", 320), ("hs1", 320), ("hv", 320), ("hc", 32), ("h1", 32),
+                       ("h2", 16), ("h3", 16), ("h4", 32), ("h5", 32), ("hm", 16), ("hn", 16), ("hw", 16), ("nv", 16), ("nr", 160),
+                       ("pe", 320), ("pg", 320), ("py", 320), ("gn", 320), ("kb0", 320), ("kb1", 320), ("kb2", 320), ("kb3", 320),
+                       ("pls", 20), ("plo", 20), ("er", 320), ("e1", 8), ("e2", 8), ("ef", 8), ("l1", 20), ("l2", 20), ("l3", 20), ("lkf", 320), ("lw", 448), ("own", 20)]),
+    "il": ("int32", [("ri", 20), ("rj", 20), ("ti", 20), ("tj", 20), ("hi", 16), ("hj", 16), ("hk", 16), ("fi", 320), ("fj", 320), ("li", 20), ("lj", 20)]),
+    "bz": ("bfloat16", [("zg0", 320), ("zg1", 320), ("zg2", 320), ("zg3", 320)]),
+    "uo": ("uint16", [("rl", 20), ("ru", 20), ("e4", 32), ("l3u", 20), ("es0", 8), ("es1", 8), ("es2", 8), ("sel0", 20), ("sel1", 20), ("sel2", 20),
+                      ("lst0", 20), ("lst1", 20), ("lst2", 20)]),
+    "bl": ("bfloat16", [("dump0", 320), ("dump1", 320), ("hx", 320), ("cf", 320), ("ceq", 320), ("cw", 320), ("cx", 320), ("gone", 320)]),
+}
+POS, SCRATCH = {}, {}
+for _a, (_d, _l) in ARENA.items():
+    _o = 0
+    for _n, _w in _l:
+        POS[_n] = (_a, _o, _w)
+        _o += (_w + 15) // 16 * 16
+    SCRATCH[_a] = ("sbuf", [128, _o], _d)
+for _n, _w in (("xt", 1280), ("ut", 512), ("vt", 512), ("kt", 4112), ("TB", 1280), ("eq", 320), ("TS", 6400), ("TO", 6400), ("TD", 1280), ("fw", 1280), ("zt", 1280), ("ett", 512), ("rt", 512)):
+    SCRATCH[_n] = ("sbuf", [128, _w], "bfloat16")
+for _n, _w in (("alt", 32), ("lxs", 32), ("lxo", 32), ("ca", 32), ("cb", 32), ("ct", 32), ("cu", 32), ("a6", 32), ("tt", 32), ("sa", 32), ("st", 32), ("la", 32), ("lt", 32),
+               ("v6", 6), ("thx", 6), ("y1", 6), ("wqt", 6), ("y4", 3)):
+    SCRATCH[_n] = ("sbuf", [128, 20, _w], "float32")
+SCRATCH["ea"] = ("sbuf", [128, 8, 32], "float32")
+SCRATCH["et"] = ("sbuf", [128, 8, 32], "float32")
+SCRATCH["olt"] = ("sbuf", [128, 20], "int32")
+for _q, _s, _w in [("uq", "us", 128), ("vq", "vs", 128), ("upq", "ups", 896), ("wq", "wsp", 512), ("kq", "ks", 1920), ("bq", "bs", 320), ("sq", "ss", 1600), ("oq", "osq", 1600), ("dq", "ds", 320)] \
+        + [("xq%d" % _t, "xs%d" % _t, 320) for _t in range(R + 1)] + [("zq%d" % _t, "zs%d" % _t, 448) for _t in range(R)] \
+        + [("hq%d" % _t, "hp%d" % _t, 128) for _t in range(R)] + [("aq%d" % _t, "ap%d" % _t, 128) for _t in range(R)]:
+    SCRATCH[_q] = ("sbuf", [128, _w], F8)
+    SCRATCH[_s] = ("sbuf", [128, _w], "uint8")
+for _t in range(R):
+    SCRATCH["eland%d" % _t] = ("sbuf", [128, 8], "uint16")
+for _b in range(8):
+    SCRATCH["ps%d" % _b] = ("psum", [128, 512], "float32")
+SEMAPHORES = ["sv", "sa", "st", "sg", "rloc"] + ["d%d" % i for i in range(NSEM)] + ["%s%d" % (k, t) for k in ("lA", "cA", "pA") for t in range(R)]
+
+
+def rank_program(g, core, T, topo):
+    rank = T.rank_of(core)
+    if rank is None:
+        return
+    nxt = T.cores[(rank + 1) % len(T.cores)]
+    prv = T.cores[(rank - 1) % len(T.cores)]
+    OP, AF = AluOpType, ActivationFunctionType
+    Q = {"v": g.vector, "a": g.scalar, "t": g.tensor, "g": g, "s": g.sync}
+    cnt = {"v": 0, "a": 0, "t": 0, "g": 0}
+    know = {q: {} for q in Q}
+    snap, lw, rd, acc, ndma = {}, {}, {}, {}, [0]
+
+    def wait(q, toks):
+        need = {}
+        for s, v_ in toks:
+            if know[q].get(s, 0) < v_:
+                need[s] = max(need.get(s, 0), v_)
+        for s in list(need):
+            for s2, v2 in need.items():
+                if s2 != s and v2 and snap.get((s2, v2), {}).get(s, 0) >= need[s]:
+                    need[s] = 0
+                    break
+        for s, v_ in need.items():
+            if v_:
+                Q[q].wait_ge(T.sem[s], v_)
+                know[q][s] = v_
+                for a, b in snap.get((s, v_), {}).items():
+                    know[q][a] = max(know[q].get(a, 0), b)
+
+    def op(q, f, r="", w="", dma=False):
+        own = "s" + q
+        toks = []
+        r, w = r.split(), w.split()
+        for k in r + w:
+            if k[:2] == "ps":
+                toks += [x for x in acc.get(k, {}).values() if x[0] != own]
+        for k in r:
+            toks += lw.get(k, [])
+        for k in w:
+            toks += [x for x in lw.get(k, []) + rd.get(k, []) if x[0] != own or k not in APART]
+        wait(q, toks)
+        ins = f()
+        if dma:
+            s, n = "d%d" % ndma[0], 16
+            ndma[0] += 1
+        else:
+            cnt[q] += 1
+            s, n = own, cnt[q]
+        ins.then_inc(T.sem[s], 16 if dma else 1)
+        snap[(s, n)] = dict(know[q])
+        tok = (s, n)
+        for k in r + w:
+            if k[:2] == "ps":
+                acc.setdefault(k, {})[s] = tok
+        for k in r:
+            rd[k] = [x for x in rd.get(k, []) if x[0] != s] + [tok]
+        for k in w:
+            lw[k] = [tok]
+            rd[k] = []
+        return tok
+
+    vec, act = g.vector, g.scalar
+
+    def v(name, a=0, b=None, p=None):
+        ar, o, n = POS[name]
+        b = n if b is None else b
+        return T[ar][:, o + a:o + b] if p is None else T[ar][p[0]:p[1], o + a:o + b]
+
+    def V(f, r="", w=""):
+        return op("v", f, r, w)
+
+    def cp(out, in_, r, w):
+        V(lambda: vec.tensor_copy(out, in_), r, w)
+
+    def ts(out, a, s1, s2, o1, o2, r, w):
+        if o2 is None:
+            V(lambda: vec.tensor_scalar(out, a, s1, None, o1), r, w)
+        else:
+            V(lambda: vec.tensor_scalar(out, a, s1, s2, o1, o2), r, w)
+
+    def tt(out, a, b, o, r, w):
+        V(lambda: vec.tensor_tensor(out, a, b, o), r, w)
+
+    def tr(out, in_, r, w):
+        V(lambda: vec.transpose(out, in_), r, w)
+
+    def fill(ap, c, w):
+        V(lambda: vec.memset(ap, c), "", w)
+
+    def ac(out, in_, r, w, func=AF.Copy, **kw):
+        op("a", lambda: act.activation(out, in_, func, **kw), r, w)
+
+    def quant(q, s, t_, r, w):
+        V(lambda: vec.quantize_mx(q, s, t_), r, w)
+
+    def mm(bank, n, L, M, r, start=True, stop=True):
+        op("t", lambda: g.tensor.matmul_mx(T["ps%d" % bank][:, 0:n], L[0], L[1], M[0], M[1], start, stop), r, "ps%d" % bank)
+
+    def iota(ap, pat, base, w, fl=False, cm=0):
+        op("g", lambda: g.iota(ap, pat, base, cm, **({"allow_small_or_imprecise_dtypes": True} if fl else {})), "", w)
+
+    def load(dst, src, w):
+        op("s", lambda: g.sync.dma_start(dst, src), "", w, dma=True)
+
+    def store(dst, src, r):
+        op("s", lambda: g.sync.dma_start(dst, src), r, "", dma=True)
+
+    def ps(b, n=320):
+        return T["ps%d" % b][:, 0:n]
+
+    def pair(q, s, a, n):
+        return (T[q][:, a:a + n], T[s][:, a:a + n])
+
+    def kst(name):
+        return pair("kq", "ks", 128 * KEYS.index(name), 128)
+
+    def ust(name):
+        return pair("upq", "ups", 128 * USEG.index(name), 128)
+
+    def pcol(i):
+        return v("pf", i, i + 1)
+    Q16, P32, PAR, ME, MO, PG, PF, BE, BO, TBI = range(10)
+
+    load(T.ut[:], T.u[:], "ut")
+    load(T.xt[:], T.x[:], "xt")
+    load(T.olt[:], T.ol[:], "olt")
+    load(T.wq[:].bitcast(dt.uint8), T.wc[:], "wq")
+    load(T.wsp[:], T.ws[:], "wsp")
+    load(T.vt[:], T.v[:], "vt")
+    for i, (pat, base) in enumerate([([[0, 8]], 8), ([[16, 8]], 0), ([[32, 4], [0, 2]], 0), ([[32, 4], [0, 2]], 16), ([[16, 8]], 1), ([[32, 4], [0, 2]], 1), ([[32, 4], [0, 2]], 17)]):
+        iota(v("uli", 8 * i, 8 * i + 8), pat, base, "uli")
+    iota(v("pii", 0, 1), [[0, 1]], 0, "p0", cm=1)
+    iota(v("ci"), [[0, 20], [1, 16]], 0, "ci", True)
+    iota(v("iof"), [[1, 320]], 0, "iof", True)
+    iota(v("cg", 0, 128), [[2, 4], [0, 32]], 0, "cg", True)
+    iota(v("cg", 128, 256), [[2, 4], [0, 32]], 1, "cg", True)
+    iota(v("inm", 0, 6), [[-1, 6]], 6, "inm", True)
+    iota(v("b16"), [[16, 20]], 0, "b16", True)
+    iota(T.wqt[:], [[0, 20], [-1, 6]], 6, "wqt", True)
+    iota(v("eli"), [[1, 10], [0, 2]], 0, "eli")
+
+    fill(v("zb"), 0.0, "zb")
+    fill(v("rss"), 0.0, "rss")
+    fill(v("rso"), 0.0, "rso")
+    fill(v("own"), 0.0, "own0")
+    cp(v("ul"), v("uli"), "uli", "ul")
+    ts(v("pii", 1, 2), v("pii", 0, 1), 15, None, OP.bitwise_and, None, "p0", "p1")
+    ts(v("pii", 2, 3), v("pii", 0, 1), 31, None, OP.bitwise_and, None, "p0", "p2")
+    ts(v("pii", 4, 5), v("pii", 0, 1), 4, None, OP.logical_shift_right, None, "p0", "p4")
+    ts(v("pii", 3, 4), v("pii", 4, 5), 1, None, OP.bitwise_and, None, "p4", "p3")
+    for d, s in ((Q16, 1), (P32, 2), (PG, 4), (PF, 0), (PAR, 3)):
+        cp(pcol(d), v("pii", s, s + 1), "p%d" % s, "pf%d" % d)
+    ts(pcol(ME), pcol(PAR), -1.0, 1.0, OP.mult, OP.add, "pf2", "pf3")
+    cp(pcol(MO), pcol(PAR), "pf2", "pf4")
+    ts(pcol(BE), pcol(ME), BIG, None, OP.mult, None, "pf3", "pf7")
+    ts(pcol(BO), pcol(MO), BIG, None, OP.mult, None, "pf4", "pf8")
+    ts(v("ms"), v("ci"), pcol(Q16), pcol(BE), OP.is_ge, OP.mult, "ci pf0 pf7", "ms")
+    quant(T.uq[:], T.us[:], T.ut[:], "ut", "uq")
+    V(lambda: vec.tensor_copy(T.upq[:].bitcast(dt.uint32), T.uq[:].bitcast(dt.uint32).indirect(v("ul"))), "uq ul", "upq")
+    ac(T.ups[:], T.us[:].indirect(v("ul")), "uq ul", "ups")
+    quant(T.xq0[:], T.xs0[:], T.xt[:], "xt", "xq0")
+    ts(v("m1"), v("ci"), pcol(Q16), pcol(BO), OP.is_le, OP.mult, "ci pf0 pf8", "m1")
+    tt(v("ms"), v("ms"), v("m1"), OP.add, "ms m1", "ms")
+    fill(T.TB[:], 0.0, "TB")
+    fill(T.eq[:], 0.0, "eq")
+    for m in range(4, -1, -1):
+        ac(T.TS[:, 1280 * m:1280 * m + 4 * NT[m]], v("zb", 0, 4 * NT[m]), "zb", "TS%d" % m)
+
+    def consts_births():
+        fill(T.kt[:, 0:512], 512.0, "kt0")
+        quant(*kst("KB"), T.kt[:, 0:512], "kt0", "kB")
+        fill(T.kt[:, 512:2064], 0.0, "kt1")
+        fill(T.kt[:, 3088:3604], 0.0, "kt2")
+        ts(T.kt[:, 3091:3603:4], v("iof", 0, 128), pcol(PF), 0.5, OP.is_equal, OP.mult, "iof pf6", "kt2")
+        ts(T.kt[:, 515:1027:4], v("iof", 0, 128), pcol(PF), 128.0, OP.is_equal, OP.mult, "iof pf6", "kt1")
+        for b in range(4):
+            quant(*kst("KH%d" % b), T.kt[:, 3091 - b:3603 - b], "kt2", "kH%d" % b)
+        ts(v("mo"), v("ms"), -1.0, None, OP.mult, None, "ms", "mo")
+
+    def consts_order():
+        for m in range(4, -1, -1):
+            fill(T.TO[:, 1280 * m:1280 * m + 4 * NT[m]], 0.0, "TO%d" % m)
+        ts(v("inm", 0, 6), v("inm", 0, 6), pcol(Q16), None, OP.is_equal, None, "inm pf0", "inm")
+        ts(v("inm", 8, 14), v("inm", 0, 6), -1.0, None, OP.add, None, "inm", "inb")
+
+    def consts_reading():
+        for i, n in enumerate("eo"):
+            m = v("gmk", 128 * i, 128 * i + 128)
+            ts(m, v("cg", 128 * i, 128 * i + 128), pcol(PG), None, OP.is_equal, None, "cg pf5", "gm%d" % i)
+            for b in range(4):
+                cp(T.kt[:, 2064 + 512 * i + b:2064 + 512 * i + 512:4], m, "gm%d" % i, "kg%d" % i)
+            o = 1028 + 516 * i
+            for b in (2, 3):
+                cp(T.kt[:, o + b:o + 512:4], m, "gm%d" % i, "kt1")
+            quant(*kst("SD" + n), T.kt[:, o + 2:o + 514], "kt1", "kS" + n)
+            quant(*kst("OD" + n), T.kt[:, o:o + 512], "kt1", "kO" + n)
+            quant(*kst("G" + n), T.kt[:, 2064 + 512 * i:2576 + 512 * i], "kg%d" % i, "kG" + n)
+        cp(v("lst0"), T.olt[:], "olt", "L0")
+        ts(v("own"), v("own"), pcol(Q16), None, OP.add, None, "own0 pf0", "own0")
+        tt(v("own"), v("b16"), v("own"), OP.add, "b16 own0", "own")
+        ts(T.wqt[:], T.wqt[:], 262144.0, None, OP.mult, None, "wqt", "wqt")
+        fill(T.thx[:], FAR, "thx")
+        ts(v("bm"), v("ci"), pcol(Q16), None, OP.is_equal, None, "ci pf0", "bm")
+        fill(v("pk"), 0.0, "pk")
+
+    def consts_counts():
+        ts(pcol(TBI), pcol(P32), -1.0, 0.5, OP.mult, OP.add, "pf1", "pf9")
+        cp(v("el"), v("eli"), "eli", "el")
+        fill(v("hc"), 0.0, "hc")
+        fill(v("hw"), 0.0, "hw")
+        fill(v("one"), 1.0, "one")
+        quant(T.vq[:], T.vs[:], T.vt[:], "vt", "vq")
+        for b in range(4):
+            quant(*kst("KE%d" % b), T.kt[:, 515 - b:1027 - b], "kt1", "kE%d" % b)
+
+    new_links = []
+
+    def lists_of_links(t_):
+        tr(T.lt[:], T.la[:], "la0 la1", "lt")
+        ts(v("l1"), T.lt[:, :, 0], pcol(ME), None, OP.mult, None, "lt pf3", "l1")
+        ts(v("l2"), T.lt[:, :, 16], pcol(MO), None, OP.mult, None, "lt pf4", "l2")
+        tt(v("l3"), v("l1"), v("l2"), OP.add, "l1 l2", "l3")
+        tt(v("li"), v("l3"), v("own"), OP.max, "l3 own", "li")
+        ts(v("lj"), v("li"), 511, None, OP.bitwise_and, None, "li", "lj")
+        cp(v("lst%d" % (t_ + 1)), v("lj"), "lj", "L%d" % (t_ + 1))
+
+    for t in range(R):
+        X = "xq%d" % t
+        XA = pair("xq%d" % t, "xs%d" % t, 0, 320)
+        L1, LK = v("lst%d" % t), "L%d" % t
+        ux = "upq ups " + X
+
+        for b, s in ((4, "USe"), (5, "USo"), (6, "US"), (0, "UB")):
+            mm(b, 320, ust(s), XA, ux)
+        for b, o in ((1, 0), (2, 128), (3, 192)):
+            mm(b, 128, pair("xq%d" % t, "xs%d" % t, o, 128), ust("UB"), ux)
+        mm(7, 320, ust("UO"), XA, ux)
+        tt(T.alt[:, :, 0:16], ps(4), v("ms"), OP.add, "ps4 ms", "alt0")
+        tt(T.alt[:, :, 16:32], ps(5), v("ms"), OP.add, "ps5 ms", "alt1")
+        mm(4, 320, ust("UOe"), XA, ux)
+        mm(5, 320, ust("UOo"), XA, ux)
+        tr(T.lxs[:], T.alt[:], "alt0 alt1", "lxs")
+        tt(v("sl"), T.lxs[:, :, 15], T.lxs[:, :, 16], OP.min, "lxs", "sl")
+        ts(v("nsl"), v("sl"), -1.0, None, OP.mult, None, "sl", "nsl")
+        tt(T.TD[:, 0:1280:4], ps(6), T.lxs[:, :, 0:16], OP.is_ge, "ps6 lxs", "TD0")
+        tt(T.TD[:, 1:1280:4], ps(6), T.lxs[:, :, 16:32], OP.is_gt, "ps6 lxs", "TD1")
+
+        def snapshots(ms_):
+            for m in ms_:
+                n, o, d = 16 * m, 1280 * (m // 4) + m % 4, "df%d" % (m % 2)
+                ac(v(d, 0, n), ps(6, n), "ps6 nsl", d, AF.Relu, bias=v("nsl", m, m + 1))
+                ac(T.TS[:, o:o + 4 * n:4], v(d, 0, n), d, "TS%d rss" % (m // 4), AF.Sign, accum_out=v("rss", m, m + 1))
+        snapshots(range(19, EARLY - 1, -1))
+        if new_links:
+            lists_of_links(new_links.pop())
+        for b in (0, 1):
+            s, n = T["ps%d" % (b + 1)][:, 0:1], 128 * (b + 1)
+            rr = "ps0 ps%d" % (b + 1)
+            ts(T.eq[:, 128 * b:128 * b + 128], T.ps0[:, 128 * b:128 * b + 128], s, None, OP.is_equal, None, rr, "eq")
+            ts(T.TB[:, b:4 * n:4], T.ps0[:, 0:n], s, None, OP.is_gt, None, rr, "TB")
+            ts(T.TB[:, 4 * n + b:1280:4], T.ps0[:, n:320], s, None, OP.is_ge, None, rr, "TB")
+        s = T.ps3[64:128, 0:1]
+        ts(T.eq[64:128, 256:320], T.ps0[64:128, 256:320], s, None, OP.is_equal, None, "ps0 ps3", "eq")
+        ts(T.TB[64:128, 2:1280:4], T.ps0[64:128, 0:320], s, None, OP.is_gt, None, "ps0 ps3", "TB")
+        op("g", lambda: g.affine_select(T.TB[:, 3:1024:4], T.eq[:, 0:256], [[0, 2], [1, 128]], OP.is_gt, 0.0, 0, -1), "eq", "TBa")
+        op("g", lambda: g.affine_select(T.TB[:, 1027:1280:4], T.eq[:, 256:320], [[1, 64]], OP.is_gt, 0.0, 64, -1), "eq", "TBb")
+        if t == 0:
+            consts_births()
+        tt(T.alt[:, :, 0:16], ps(4), v("mo"), OP.add, "ps4 mo", "alt0")
+        tt(T.alt[:, :, 16:32], ps(5), v("mo"), OP.add, "ps5 mo", "alt1")
+        quant(T.bq[:], T.bs[:], T.TB[:], "TB TBa TBb", "bq")
+        mm(0, 320, kst("KB"), (T.bq[:], T.bs[:]), "kB bq")
+        for b in (1, 2, 3):
+            mm(b, 320, kst("KH%d" % b), XA, "kH%d %s" % (b, X))
+        tr(T.lxo[:], T.alt[:], "alt0 alt1", "lxo")
+        tt(v("va"), ps(0), v("iof"), OP.add, "ps0 iof", "va")
+        mm(0, 320, kst("KH0"), XA, "kH0 " + X)
+        tt(v("slo"), T.lxo[:, :, 15], T.lxo[:, :, 16], OP.max, "lxo", "slo")
+        tt(T.TD[:, 2:1280:4], ps(7), T.lxo[:, :, 0:16], OP.is_le, "ps7 lxo", "TD2")
+        tt(T.TD[:, 3:1280:4], ps(7), T.lxo[:, :, 16:32], OP.is_lt, "ps7 lxo", "TD3")
+        if t == 0:
+            consts_order()
+        for i in range(6):
+            ac(v("inj", 320 * i, 320 * i + 320), v("va"), "va inm inb", "inj%d" % i, AF.Identity, bias=v("inm", 8 + i, 9 + i), scale=v("inm", i, i + 1))
+        for b in (3, 1, 2, 0):
+            ac(T.fw[:, 320 * b:320 * b + 320], ps(b), "ps%d" % b, "fw%d" % b)
+        mm(5, 320, ust("UO"), XA, ux)
+        snapshots(range(EARLY - 1, 0, -1))
+        for m in range(19, 0, -1):
+            if m not in ACT_ORDER:
+                n, o = 16 * m, 1280 * (m // 4) + m % 4
+                ts(T.TO[:, o:o + 4 * n:4], ps(7, n), v("slo", m, m + 1), None, OP.is_lt, None, "ps7 slo", "TO%d o%d" % (m // 4, m))
+        if t == 0:
+            consts_reading()
+        quant(T.dq[:], T.ds[:], T.TD[:], "TD0 TD1 TD2 TD3", "dq")
+        for m in range(19, 0, -1):
+            n, o, d = 16 * m, 1280 * (m // 4) + m % 4, "df%d" % (m % 2)
+            if m in ACT_ORDER:
+                ac(v(d, 0, n), ps(5, n), "ps5 slo", d, AF.Relu, bias=v("slo", m, m + 1), scale=-1.0)
+                ac(T.TO[:, o:o + 4 * n:4], v(d, 0, n), d, "TO%d rso" % (m // 4), AF.Sign, accum_out=v("rso", m, m + 1))
+        for m in range(19, 0, -1):
+            n, o = 16 * m, 1280 * (m // 4) + m % 4
+            if m not in ACT_ORDER:
+                d = "dump%d" % (m % 2)
+                ac(v(d, 0, n), T.TO[:, o:o + 4 * n:4], "o%d" % m, d + " rso", AF.Copy, accum_out=v("rso", m, m + 1))
+        if t == 0:
+            for k in range(10):
+                o = 352 * k
+                ac(v("pk", o, o + 16), v("bm", 0, 16), "bm", "pk")
+                ac(v("pk", o + 16, o + 32), v("bm", 0, 16), "bm", "pk", scale=4096.0)
+
+        src, sk = v("inj", 0, 320), "inj0"
+        for i in range(1, 6):
+            d = "aw%d" % (i % 2)
+            tt(v(d), src.indirect(L1), v("inj", 320 * i, 320 * i + 320), OP.max, "%s inj%d %s" % (sk, i, LK), d)
+            src, sk = v(d), d
+        ac(v("a6f"), src.indirect(L1), "%s %s" % (sk, LK), "a6f")
+        ac(T.a6[:, :, 0:16], v("a6f"), "a6f", "a60")
+        ac(T.a6[:, :, 16:32], v("a6f"), "a6f", "a61")
+
+        def sums(tile, q, s, key, banks, pre):
+            for i, n in enumerate("eo"):
+                mm(banks[i], 320, kst(pre + n), (T.dq[:], T.ds[:]), "k%s%s dq" % (pre[0], n), True, False)
+            for m in range(4, -1, -1):
+                p = pair(q, s, 320 * m, NT[m])
+                quant(p[0], p[1], T[tile][:, 1280 * m:1280 * m + 4 * NT[m]], "%s%d" % (key, m), "q%s%d" % (key, m))
+                for i, n in enumerate("eo"):
+                    mm(banks[i], NT[m], kst("G" + n), p, "kG%s q%s%d" % (n, key, m), False, m == 0)
+
+        sums("TS", "sq", "ss", "TS", (4, 6), "SD")
+        sums("TO", "oq", "osq", "TO", (5, 7), "OD")
+        tt(v("pls"), v("b16"), v("rss"), OP.subtract, "b16 rss", "pls")
+        tr(T.tt[:], T.a6[:], "a60 a61", "tt")
+        ts(T.v6[:], T.tt[:, :, 1:7], pcol(ME), None, OP.mult, None, "tt pf3", "v6")
+        ts(T.y1[:], T.tt[:, :, 17:23], pcol(MO), None, OP.mult, None, "tt pf4", "y1")
+        tt(T.v6[:], T.v6[:], T.y1[:], OP.add, "v6 y1", "v6")
+        cp(v("ti"), T.v6[:, :, 2], "v6", "ti")
+        ts(v("tj"), v("ti"), 511, None, OP.bitwise_and, None, "ti", "tj")
+        cp(v("l3u"), v("tj"), "tj", "l3u")
+        ac(T.cb[:, :, 0:16], ps(4), "ps4", "cb0")
+        ac(T.cb[:, :, 16:32], ps(6), "ps6", "cb1")
+        tr(T.cu[:], T.cb[:], "cb0 cb1", "cu")
+        tt(v("pls"), v("pls"), T.cu[:, :, 0], OP.add, "pls cu", "pls")
+        for i in range(5):
+            ac(T.thx[:, :, i], v("pls"), "pls", "thx", AF.Copy, scale=512.0, bias=512.0)
+        tt(T.y1[:], T.v6[:], T.thx[:], OP.is_lt, "v6 thx", "y1")
+        tt(T.y1[:], T.y1[:], T.wqt[:], OP.mult, "y1 wqt", "y1")
+        tt(T.y1[:], T.y1[:], T.v6[:], OP.add, "y1 v6", "y1")
+        tt(T.y4[:], T.y1[:, :, 0:3], T.y1[:, :, 3:6], OP.max, "y1", "y4")
+        tt(v("y5"), T.y4[:, :, 0], T.y4[:, :, 1], OP.max, "y4", "y5")
+        tt(v("ri"), v("y5"), T.y4[:, :, 2], OP.max, "y5 y4", "ri")
+        ts(v("rj"), v("ri"), 511, None, OP.bitwise_and, None, "ri", "rj")
+        cp(v("rl"), v("rj"), "rj", "rl")
+        if t == 0:
+            consts_counts()
+        for k in range(10 - VEC_COUNTS):
+            if k == GATHER_AT:
+                for b in range(4):
+                    ac(v("zg%d" % b), T.fw[:, 320 * b:320 * b + 320].indirect(v("rl")), "fw%d rl" % b, "zg%d" % b)
+            d = "hs%d" % (k % 2)
+            ac(v(d), v("pk", 320 * k, 320 * k + 320).indirect(v("rl")), "pk rl", d + " hc", AF.Copy, accum_out=v("hc", k, k + 1))
+        cp(T.ca[:, :, 0:16], ps(5), "ps5", "ca0")
+        cp(T.ca[:, :, 16:32], ps(7), "ps7", "ca1")
+        tr(T.ct[:], T.ca[:], "ca0 ca1", "ct")
+        tt(v("plo"), v("b16"), v("rso"), OP.subtract, "b16 rso", "plo")
+        tt(v("plo"), v("plo"), T.ct[:, :, 0], OP.add, "plo ct", "plo")
+        cp(v("ru"), v("plo"), "plo", "ru")
+        V(lambda: vec.tensor_copy(v("er").indirect(v("ru")), v("iof")), "ru iof", "er")
+        cp(T.ea[:, :, 0:16], v("er", 0, 128), "er", "ea0")
+        cp(T.ea[:, :, 16:32], v("er", 0, 128), "er", "ea1")
+        tr(T.et[:], T.ea[:], "ea0 ea1", "et")
+        ts(v("e1"), T.et[:, :, 0], pcol(ME), None, OP.mult, None, "et pf3", "e1")
+        ts(v("e2"), T.et[:, :, 16], pcol(MO), None, OP.mult, None, "et pf4", "e2")
+        tt(v("ef"), v("e1"), v("e2"), OP.add, "e1 e2", "ef")
+        for i in range(4):
+            ts(v("e4", 8 * i, 8 * i + 8), v("ef"), 4.0, float(i), OP.mult, OP.add, "ef", "e4")
+        cp(v("es%d" % t), v("ef"), "ef", "es%d" % t)
+        for b in range(4):
+            tt(T.zt[:, b:1280:4], ps(b), v("zg%d" % b), OP.add, "ps%d zg%d" % (b, b), "zt%d" % b)
+        zk = "zt0 zt1 zt2 zt3"
+        for b in range(4):
+            V(lambda: vec.tensor_copy(T.ett[:, b:512:4], T.zt[:].indirect(v("e4", 8 * b, 8 * b + 8))), zk + " e4", "ett%d" % b)
+        HQ = pair("hq%d" % t, "hp%d" % t, 0, 128)
+        quant(HQ[0], HQ[1], T.ett[:], "ett0 ett1 ett2 ett3", "hE%d" % t)
+        rid, pid = topo.addr(nxt)[0:2]
+        eng = topo.engines(core, nxt)
+        h = len(eng) // 2
+        m1, m2 = sum(1 << e for e in eng[:h]), sum(1 << e for e in eng[h:])
+
+        def send(dst, src_, sem, mask, key):
+            wait("g", lw[key])
+            g.remote_dma(dst, src_, T.sem[sem + str(t)], T.sem.rloc, pid, rid, mask)
+        send(T["eland%d" % t][:], v("es%d" % t), "lA", m2, "es%d" % t)
+        send(T["aq%d" % t][:].bitcast(dt.uint8), T["hq%d" % t][:].bitcast(dt.uint8), "cA", m1, "hE%d" % t)
+        send(T["ap%d" % t][:], T["hp%d" % t][:], "pA", m2, "hE%d" % t)
+        he = topo.engines(prv, core)
+        for s, k, n in (("lA", "eland%d" % t, len(he) - len(he) // 2), ("cA", "aq%d" % t, len(he) // 2), ("pA", "ap%d" % t, len(he) - len(he) // 2)):
+            lw[k] = [(s + str(t), n)]
+        zq, zs = T["zq%d" % t], T["zs%d" % t]
+        quant(zq[:, 0:320], zs[:, 0:320], T.zt[:], zk, "zqa%d" % t)
+        for k in range(10 - VEC_COUNTS, 10):
+            cp(v("hv"), v("pk", 320 * k, 320 * k + 320).indirect(v("rl")), "pk rl", "hv")
+            V(lambda: vec.tensor_reduce(v("hc", k, k + 1), v("hv"), AxisListType.X, OP.add), "hv", "hd")
+
+        tr(v("h1"), v("hc"), "hc" + (" hd" if VEC_COUNTS else ""), "h1")
+        tt(v("h2"), v("h1", 0, 16), v("h1", 16, 32), OP.add, "h1", "h2")
+        tt(v("h3", 0, 16, (0, 32)), v("h2", 0, 16, (0, 32)), v("h2", 0, 16, (32, 64)), OP.add, "h2", "h3a")
+        tt(v("h3", 0, 16, (64, 96)), v("h2", 0, 16, (64, 96)), v("h2", 0, 16, (96, 128)), OP.add, "h2", "h3b")
+        for a in range(4):
+            tt(v("h4", 0, 16, (32 * a, 32 * a + 32)), v("h3", 0, 16, (0, 32)), v("h3", 0, 16, (64, 96)), OP.add, "h3a h3b", "h4")
+        cp(v("h4", 16, 32), v("h4", 0, 16), "h4", "h4b")
+        tr(v("h5"), v("h4"), "h4 h4b", "h5")
+        cp(v("hi", 0, 10), v("h5", 0, 10), "h5", "hi")
+        ts(v("hj", 0, 10), v("hi", 0, 10), 4095, None, OP.bitwise_and, None, "hi", "hj")
+        ts(v("hk", 0, 10), v("hi", 0, 10), 12, None, OP.logical_shift_right, None, "hi", "hk")
+        ts(v("hm", 0, 10), v("hj", 0, 10), pcol(ME), 64.0, OP.mult, OP.min, "hj pf3", "hm")
+        ts(v("hn", 0, 10), v("hk", 0, 10), pcol(MO), 64.0, OP.mult, OP.min, "hk pf4", "hn")
+        tt(v("hw", 0, 10), v("hm", 0, 10), v("hn", 0, 10), OP.add, "hm hn", "hw")
+        ac(v("hx"), v("hw").indirect(v("el")), "hw el", "hx")
+        tr(v("cf"), v("hx"), "hx", "cf")
+        ac(v("dump0"), v("cf"), "cf pf9", "dump0 nv0", AF.Sign, bias=pcol(TBI), accum_out=v("nv", 0, 1))
+        ts(v("nr", 0, 32), v("one"), v("nv", 0, 1), None, OP.mult, None, "one nv0", "nr0")
+        tr(v("nr", 32, 64), v("nr", 0, 32), "nr0", "nr1")
+        ts(v("nr", 64, 96), v("nr", 32, 64), 64.0, None, OP.is_gt, None, "nr1", "nr2")
+        ts(v("nr", 96, 128), v("nr", 32, 64), 64.0, FAR, OP.is_le, OP.mult, "nr1", "nr3")
+        V(lambda: vec.tensor_reduce(v("nv", 1, 2), v("nr", 64, 96), AxisListType.X, OP.add), "nr2", "nv1")
+        tt(v("nr", 128, 160), v("nr", 96, 128), v("nr", 32, 64), OP.add, "nr3 nr1", "nr4")
+        ts(v("nv", 3, 4), v("nv", 1, 2), -1.0, None, OP.add, None, "nv1", "nv3")
+        V(lambda: vec.tensor_reduce(v("nv", 2, 3), v("nr", 128, 160), AxisListType.X, OP.min), "nr4", "nv2")
+        ts(v("ceq"), v("cf"), v("nv", 3, 4), None, OP.is_equal, None, "cf nv3", "ceq")
+        ts(v("nv", 4, 5), v("nv", 2, 3), 0.5, -32.0, OP.mult, OP.add, "nv2", "nv4")
+        V(lambda: vec.tensor_tensor_scan(v("pe"), v("ceq"), v("zb", 0, 320), 0.0, OP.add, OP.max), "ceq zb", "pe")
+        ts(v("cw"), v("pe"), v("nv", 4, 5), 0.5, OP.is_gt, OP.mult, "pe nv4", "cw")
+        tt(v("cx"), v("cf"), v("cw"), OP.add, "cf cw", "cx")
+        ts(v("gone"), v("cx"), v("nv", 3, 4), None, OP.is_le, None, "cx nv3", "gone")
+        V(lambda: vec.tensor_tensor_scan(v("pg"), v("gone"), v("zb", 0, 320), 319.0, OP.add, OP.max), "gone zb", "pg")
+        ac(v("gn"), v("gone"), "gone", "gn", AF.Copy, scale=-FAR)
+        tt(v("py"), v("pg"), v("gone"), OP.mult, "pg gone", "py")
+        tt(T.sa[:, :, 0:16], v("py"), v("iof"), OP.max, "py iof", "sa0")
+        ac(T.sa[:, :, 16:32], T.sa[:, :, 0:16], "sa0", "sa1")
+        tt(v("kb0"), v("gn"), v("iof"), OP.add, "gn iof", "kb0")
+        tr(T.st[:], T.sa[:], "sa0 sa1", "st")
+        sel = v("sel%d" % t)
+        cp(sel, T.st[:, :, 0], "st", "sel%d" % t)
+
+        AQ = pair("aq%d" % t, "ap%d" % t, 0, 128)
+        ak = "aq%d ap%d " % (t, t)
+        for b in range(4):
+            mm(4 + b, 128, pair("wq", "wsp", 128 * b, 128), AQ, "wq wsp " + ak, True, False)
+            mm(4 + b, 128, kst("KE%d" % b), AQ, "kE%d %s" % (b, ak), False, True)
+        for b in range(4):
+            o = T.rt[:, b:512:4]
+            if b % 2 == 0:
+                ac(o, ps(4 + b, 128), "ps%d" % (4 + b), "rt%d" % b, scale=0.0078125)
+            else:
+                ts(o, ps(4 + b, 128), 0.0078125, None, OP.mult, None, "ps%d" % (4 + b), "rt%d" % b)
+        quant(zq[:, 320:448], zs[:, 320:448], T.rt[:], "rt0 rt1 rt2 rt3", "zqb%d" % t)
+        nx = "xq%d" % (t + 1)
+        nq, ns = T[nx], T["xs%d" % (t + 1)]
+        zz = "zqa%d zqb%d sel%d" % (t, t, t)
+        V(lambda: vec.tensor_copy(nq[:].bitcast(dt.uint32), zq[:].bitcast(dt.uint32).indirect(sel)), zz, nx + "c")
+        op("a", lambda: act.activation(ns[:], zs[:].indirect(sel), AF.Copy), zz, nx + "s")
+        lw[nx] = lw[nx + "c"] + lw[nx + "s"]
+        if t == R - 1:
+            mm(0, 320, (T.vq[:], T.vs[:]), (nq[:], ns[:]), "vq " + nx)
+            store(T.oc[:], nq[:].bitcast(dt.uint8), nx)
+            for k in range(4):
+                store(T.osc[4 * k:4 * k + 4, :], ns[32 * k:32 * k + 4, :], nx)
+
+        for i in range(1, 4):
+            ac(v("kb%d" % i), v("kb0"), "kb0", "kb%d" % i, AF.Copy, bias=512.0 * i)
+        tt(v("aw0"), v("kb1").indirect(L1), v("kb2"), OP.max, "kb1 kb2 " + LK, "aw0")
+        tt(v("aw1"), v("aw0").indirect(L1), v("kb3"), OP.max, "aw0 kb3 " + LK, "aw1")
+        ac(v("lw", 320, 448), v("iof").indirect(T["eland%d" % t][:]), "iof eland%d" % t, "lw1", AF.Copy, bias=512.0)
+        ac(v("dw"), v("aw1").indirect(L1), "aw1 " + LK, "dw")
+        ac(v("dx"), v("dw"), "dw", "dx", AF.Copy, bias=2048.0)
+        tt(v("lw", 0, 320), v("dw").indirect(v("l3u")), v("dx"), OP.max, "dw dx l3u", "lw0")
+        lsrc = v("lw").indirect(sel)
+        if t == R - 1:
+            ac(v("hs0"), ps(0), "ps0", "hs0")
+            store(T.y[:], v("hs0"), "hs0")
+            cp(v("lkf"), lsrc, "lw0 lw1 sel%d" % t, "lkf")
+            tt(v("fi"), v("lkf"), v("iof"), OP.max, "lkf iof", "fi")
+            ts(v("fj"), v("fi"), 511, None, OP.bitwise_and, None, "fi", "fj")
+            cp(v("lkf"), v("fj"), "fj", "lkf")
+            store(T.lk[:], T.fl[0:128:16, POS["lkf"][1]:POS["lkf"][1] + 320], "lkf")
+        else:
+            ac(v("lkf"), lsrc, "lw0 lw1 sel%d" % t, "lkf")
+            ac(T.la[:, :, 0:16], v("lkf"), "lkf", "la0")
+            ac(T.la[:, :, 16:32], v("lkf"), "lkf", "la1")
+            new_links.append(t)
+    for q in ("v", "a", "t", "g"):
+        g.wait_ge(T.sem["s" + q], cnt[q])
+    for i in range(ndma[0]):
+        g.wait_ge(T.sem["d%d" % i], 16)
+    g.wait_ge(T.sem.rloc, R * (h + 2 * (len(eng) - h)))

@@ -14,6 +14,13 @@ VEC_COUNTS = 1
 
 APART = ["TB", "eq", "rss", "rso", "hc", "hd", "thx", "e4", "pk", "h4", "kg0", "kg1"] + ["TS%d" % _m for _m in range(5)] + ["TO%d" % _m for _m in range(5)] + ["ps%d" % _m for _m in range(8)]
 
+CYCLE, WAKE = 0.00103, 0.1
+SIZE = {_k: 640 for _k in "lxs lxo tt ct cu st lt".split()}
+SIZE.update({_k: 64 for _k in ("p1 p2 p3 p4 sl nsl slo pls plo ru y4 y5 ri rj rl ti tj l3u e1 e2 ef e4 es0 es1 es2 h1 h2 h3a h3b h4 h4b h5 hi hj hk hm hn hw nr0 nr1 nr2 nr3 nr4 "
+                              "nv1 nv2 nv3 nv4 sel0 sel1 sel2 l1 l2 l3 li lj L0 L1 L2 thx own own0 inm inb rss rso hc").split()})
+SIZE.update({"pf%d" % _k: 64 for _k in range(10)})
+SIZE.update({"v6": 120, "y1": 120, "ea0": 128, "ea1": 128, "et": 256, "lw1": 200, "pk": 64, "gm0": 128, "gm1": 128, "kg0": 128, "kg1": 128, "kt1": 128})
+
 F8 = "float8_e4m3fn_x4"
 ARENA = {
     "fc": ("float32", [("pf", 16), ("iof", 320), ("ci", 320), ("cg", 256), ("ms", 320), ("mo", 320), ("m1", 320), ("inm", 16), ("b16", 20), ("one", 32)]),
@@ -68,7 +75,7 @@ def rank_program(g, core, T, topo):
     Q = {"v": g.vector, "a": g.scalar, "t": g.tensor, "g": g, "s": g.sync}
     cnt = {"v": 0, "a": 0, "t": 0, "g": 0}
     know = {q: {} for q in Q}
-    snap, lw, rd, acc, ndma = {}, {}, {}, {}, [0]
+    snap, lw, rd, acc, filled, ndma = {}, {}, {}, {}, {}, [0]
 
     def wait(q, toks):
         need = {}
@@ -87,19 +94,88 @@ def rank_program(g, core, T, topo):
                 for a, b in snap.get((s, v_), {}).items():
                     know[q][a] = max(know[q].get(a, 0), b)
 
-    def op(q, f, r="", w="", dma=False):
+    ops = []
+
+    def op(q, f, r="", w="", dma=False, c=0, fill=False):
+        ops.append({"q": q, "f": f, "r": r.split(), "w": w.split(), "dma": dma, "c": c, "fill": fill, "lat": 2.0 if dma else 2.6 if q == "n" else 0.0})
+
+    def schedule():
+        n = len(ops)
+        pred = [{} for _ in ops]
+        last, reads, bank = {}, {}, {}
+        for i, o in enumerate(ops):
+            p = pred[i]
+
+            def dep(j, full=True):
+                if j != i:
+                    p[j] = p.get(j, False) or full
+            for k in o["r"] + o["w"]:
+                if k[:2] == "ps":
+                    for q2, j in bank.get(k, {}).items():
+                        dep(j, q2 != o["q"])
+            for k in o["r"]:
+                if k in last and k[:2] != "ps":
+                    dep(last[k])
+            for k in o["w"]:
+                if k[:2] != "ps":
+                    for j in ([last[k]] if k in last else []) + reads.get(k, []):
+                        dep(j, ops[j]["q"] != o["q"] or k not in APART or ops[j]["fill"])
+            for k in o["r"] + o["w"]:
+                if k[:2] == "ps":
+                    bank.setdefault(k, {})[o["q"]] = i
+            for k in o["r"]:
+                reads.setdefault(k, []).append(i)
+            for k in o["w"]:
+                if k in APART and k in last and ops[last[k]]["q"] == o["q"] and not reads.get(k):
+                    dep(last[k], ops[last[k]]["fill"])
+                last[k], reads[k] = i, []
+        prio = [0.0] * n
+        for i in range(n - 1, -1, -1):
+            prio[i] += ops[i]["c"] + ops[i]["lat"]
+            for j, full in pred[i].items():
+                prio[j] = max(prio[j], prio[i] + (WAKE if full else 0.0))
+        succ, left, ready = [[] for _ in ops], [len(p) for p in pred], [0.0] * n
+        for i, p in enumerate(pred):
+            for j, full in p.items():
+                succ[j].append((i, full))
+        free = {q: 0.0 for q in list(Q) + ["n"]}
+        pool = {q: [] for q in free}
+        for i in range(n):
+            if not left[i]:
+                pool[ops[i]["q"]].append(i)
+        order = []
+        while len(order) < n:
+            best = min((max(free[q], min(ready[i] for i in pool[q])), q) for q in pool if pool[q])
+            start, q = best
+            i = max((x for x in pool[q] if ready[x] <= start + 1e-9), key=lambda x: prio[x])
+            pool[q].remove(i)
+            end = start + ops[i]["c"]
+            free[q] = end if q != "n" else 0.0
+            order.append(i)
+            for j, full in succ[i]:
+                ready[j] = max(ready[j], end + ops[i]["lat"] + WAKE if full else start)
+                left[j] -= 1
+                if not left[j]:
+                    pool[ops[j]["q"]].append(j)
+        return order
+
+    def emit(q, f, r, w, dma, fill):
         own = "s" + q
         toks = []
-        r, w = r.split(), w.split()
+        if q == "n":
+            lw[w[0]] = [f]
+            return
         for k in r + w:
             if k[:2] == "ps":
                 toks += [x for x in acc.get(k, {}).values() if x[0] != own]
         for k in r:
             toks += lw.get(k, [])
         for k in w:
-            toks += [x for x in lw.get(k, []) + rd.get(k, []) if x[0] != own or k not in APART]
+            toks += [x for x in lw.get(k, []) + rd.get(k, []) if x[0] != own or k not in APART] + filled.get(k, [])
         wait(q, toks)
         ins = f()
+        if w and w[0][:3] == "snd":
+            return
         if dma:
             s, n = "d%d" % ndma[0], 16
             ndma[0] += 1
@@ -117,7 +193,8 @@ def rank_program(g, core, T, topo):
         for k in w:
             lw[k] = [tok]
             rd[k] = []
-        return tok
+            if fill:
+                filled[k] = [tok]
 
     vec, act = g.vector, g.scalar
 
@@ -126,44 +203,51 @@ def rank_program(g, core, T, topo):
         b = n if b is None else b
         return T[ar][:, o + a:o + b] if p is None else T[ar][p[0]:p[1], o + a:o + b]
 
-    def V(f, r="", w=""):
-        return op("v", f, r, w)
+    def V(f, r, w, n=0, k=1.0):
+        n = n or SIZE.get(w.split()[0], 320)
+        op("v", f, r, w, c=CYCLE * max(64.0, n * k))
 
-    def cp(out, in_, r, w):
-        V(lambda: vec.tensor_copy(out, in_), r, w)
+    def cp(out, in_, r, w, n=0, k=1.0):
+        V(lambda: vec.tensor_copy(out, in_), r, w, n, k)
 
-    def ts(out, a, s1, s2, o1, o2, r, w):
+    def ts(out, a, s1, s2, o1, o2, r, w, n=0):
         if o2 is None:
-            V(lambda: vec.tensor_scalar(out, a, s1, None, o1), r, w)
+            V(lambda: vec.tensor_scalar(out, a, s1, None, o1), r, w, n)
         else:
-            V(lambda: vec.tensor_scalar(out, a, s1, s2, o1, o2), r, w)
+            V(lambda: vec.tensor_scalar(out, a, s1, s2, o1, o2), r, w, n)
 
     def tt(out, a, b, o, r, w):
-        V(lambda: vec.tensor_tensor(out, a, b, o), r, w)
+        V(lambda: vec.tensor_tensor(out, a, b, o), r, w, 0, 1.0 if r[:2] == "ps" else 2.0)
 
     def tr(out, in_, r, w):
         V(lambda: vec.transpose(out, in_), r, w)
 
-    def fill(ap, c, w):
-        V(lambda: vec.memset(ap, c), "", w)
+    def scan(out, a, b, c, r, w):
+        V(lambda: vec.tensor_tensor_scan(out, a, b, c, OP.add, OP.max), r, w)
 
-    def ac(out, in_, r, w, func=AF.Copy, **kw):
-        op("a", lambda: act.activation(out, in_, func, **kw), r, w)
+    def red(out, in_, o, r, w, n=0):
+        V(lambda: vec.tensor_reduce(out, in_, AxisListType.X, o), r, w, n)
 
-    def quant(q, s, t_, r, w):
-        V(lambda: vec.quantize_mx(q, s, t_), r, w)
+    def fill(ap, c, w, n=0):
+        op("v", lambda: vec.memset(ap, c), "", w, c=CYCLE * max(64.0, 0.5 * (n or SIZE.get(w, 320))), fill=True)
+
+    def ac(out, in_, r, w, func=AF.Copy, n=0, k=1.0, **kw):
+        op("a", lambda: act.activation(out, in_, func, **kw), r, w, c=CYCLE * max(64.0, k * (n or SIZE.get(w.split()[0], 320))))
+
+    def quant(q, s, t_, r, w, n=320):
+        op("v", lambda: vec.quantize_mx(q, s, t_), r, w, c=0.015 + 0.0011 * n)
 
     def mm(bank, n, L, M, r, start=True, stop=True):
-        op("t", lambda: g.tensor.matmul_mx(T["ps%d" % bank][:, 0:n], L[0], L[1], M[0], M[1], start, stop), r, "ps%d" % bank)
+        op("t", lambda: g.tensor.matmul_mx(T["ps%d" % bank][:, 0:n], L[0], L[1], M[0], M[1], start, stop), r, "ps%d" % bank, c=1.5 * CYCLE * (n + 16))
 
-    def iota(ap, pat, base, w, fl=False, cm=0):
-        op("g", lambda: g.iota(ap, pat, base, cm, **({"allow_small_or_imprecise_dtypes": True} if fl else {})), "", w)
+    def iota(ap, pat, first, w, fl=False, cm=0):
+        op("g", lambda: g.iota(ap, pat, first, cm, **({"allow_small_or_imprecise_dtypes": True} if fl else {})), "", w, c=0.3)
 
     def load(dst, src, w):
-        op("s", lambda: g.sync.dma_start(dst, src), "", w, dma=True)
+        op("s", lambda: g.sync.dma_start(dst, src), "", w, dma=True, c=0.1)
 
     def store(dst, src, r):
-        op("s", lambda: g.sync.dma_start(dst, src), r, "", dma=True)
+        op("s", lambda: g.sync.dma_start(dst, src), r, "", dma=True, c=0.1)
 
     def ps(b, n=320):
         return T["ps%d" % b][:, 0:n]
@@ -216,9 +300,9 @@ def rank_program(g, core, T, topo):
     ts(pcol(BO), pcol(MO), BIG, None, OP.mult, None, "pf4", "pf8")
     ts(v("ms"), v("ci"), pcol(Q16), pcol(BE), OP.is_ge, OP.mult, "ci pf0 pf7", "ms")
     quant(T.uq[:], T.us[:], T.ut[:], "ut", "uq")
-    V(lambda: vec.tensor_copy(T.upq[:].bitcast(dt.uint32), T.uq[:].bitcast(dt.uint32).indirect(v("ul"))), "uq ul", "upq")
-    ac(T.ups[:], T.us[:].indirect(v("ul")), "uq ul", "ups")
-    quant(T.xq0[:], T.xs0[:], T.xt[:], "xt", "xq0")
+    cp(T.upq[:].bitcast(dt.uint32), T.uq[:].bitcast(dt.uint32).indirect(v("ul")), "uq ul", "upq", 896, 1.6)
+    ac(T.ups[:], T.us[:].indirect(v("ul")), "uq ul", "ups", n=896, k=1.6)
+    quant(T.xq0[:], T.xs0[:], T.xt[:], "xt", "xq0c xq0s")
     ts(v("m1"), v("ci"), pcol(Q16), pcol(BO), OP.is_le, OP.mult, "ci pf0 pf8", "m1")
     tt(v("ms"), v("ms"), v("m1"), OP.add, "ms m1", "ms")
     fill(T.TB[:], 0.0, "TB")
@@ -285,7 +369,7 @@ def rank_program(g, core, T, topo):
         cp(v("lst%d" % (t_ + 1)), v("lj"), "lj", "L%d" % (t_ + 1))
 
     for t in range(R):
-        X = "xq%d" % t
+        X = "xq%dc xq%ds" % (t, t)
         XA = pair("xq%d" % t, "xs%d" % t, 0, 320)
         L1, LK = v("lst%d" % t), "L%d" % t
         ux = "upq ups " + X
@@ -364,6 +448,7 @@ def rank_program(g, core, T, topo):
                 d = "dump%d" % (m % 2)
                 ac(v(d, 0, n), T.TO[:, o:o + 4 * n:4], "o%d" % m, d + " rso", AF.Copy, accum_out=v("rso", m, m + 1))
         if t == 0:
+            consts_counts()
             for k in range(10):
                 o = 352 * k
                 ac(v("pk", o, o + 16), v("bm", 0, 16), "bm", "pk")
@@ -411,8 +496,6 @@ def rank_program(g, core, T, topo):
         tt(v("ri"), v("y5"), T.y4[:, :, 2], OP.max, "y5 y4", "ri")
         ts(v("rj"), v("ri"), 511, None, OP.bitwise_and, None, "ri", "rj")
         cp(v("rl"), v("rj"), "rj", "rl")
-        if t == 0:
-            consts_counts()
         for k in range(10 - VEC_COUNTS):
             if k == GATHER_AT:
                 for b in range(4):
@@ -425,7 +508,7 @@ def rank_program(g, core, T, topo):
         tt(v("plo"), v("b16"), v("rso"), OP.subtract, "b16 rso", "plo")
         tt(v("plo"), v("plo"), T.ct[:, :, 0], OP.add, "plo ct", "plo")
         cp(v("ru"), v("plo"), "plo", "ru")
-        V(lambda: vec.tensor_copy(v("er").indirect(v("ru")), v("iof")), "ru iof", "er")
+        cp(v("er").indirect(v("ru")), v("iof"), "ru iof", "er", 320, 3.8)
         cp(T.ea[:, :, 0:16], v("er", 0, 128), "er", "ea0")
         cp(T.ea[:, :, 16:32], v("er", 0, 128), "er", "ea1")
         tr(T.et[:], T.ea[:], "ea0 ea1", "et")
@@ -439,28 +522,28 @@ def rank_program(g, core, T, topo):
             tt(T.zt[:, b:1280:4], ps(b), v("zg%d" % b), OP.add, "ps%d zg%d" % (b, b), "zt%d" % b)
         zk = "zt0 zt1 zt2 zt3"
         for b in range(4):
-            V(lambda: vec.tensor_copy(T.ett[:, b:512:4], T.zt[:].indirect(v("e4", 8 * b, 8 * b + 8))), zk + " e4", "ett%d" % b)
+            cp(T.ett[:, b:512:4], T.zt[:].indirect(v("e4", 8 * b, 8 * b + 8)), zk + " e4", "ett%d" % b, 128, 2.0)
         HQ = pair("hq%d" % t, "hp%d" % t, 0, 128)
-        quant(HQ[0], HQ[1], T.ett[:], "ett0 ett1 ett2 ett3", "hE%d" % t)
+        quant(HQ[0], HQ[1], T.ett[:], "ett0 ett1 ett2 ett3", "hE%d" % t, 128)
         rid, pid = topo.addr(nxt)[0:2]
         eng = topo.engines(core, nxt)
         h = len(eng) // 2
         m1, m2 = sum(1 << e for e in eng[:h]), sum(1 << e for e in eng[h:])
 
         def send(dst, src_, sem, mask, key):
-            wait("g", lw[key])
-            g.remote_dma(dst, src_, T.sem[sem + str(t)], T.sem.rloc, pid, rid, mask)
+            rs = T.sem[sem + str(t)]
+            op("g", lambda: g.remote_dma(dst, src_, rs, T.sem.rloc, pid, rid, mask), key, "snd" + sem + str(t), c=0.8)
         send(T["eland%d" % t][:], v("es%d" % t), "lA", m2, "es%d" % t)
         send(T["aq%d" % t][:].bitcast(dt.uint8), T["hq%d" % t][:].bitcast(dt.uint8), "cA", m1, "hE%d" % t)
         send(T["ap%d" % t][:], T["hp%d" % t][:], "pA", m2, "hE%d" % t)
         he = topo.engines(prv, core)
         for s, k, n in (("lA", "eland%d" % t, len(he) - len(he) // 2), ("cA", "aq%d" % t, len(he) // 2), ("pA", "ap%d" % t, len(he) - len(he) // 2)):
-            lw[k] = [(s + str(t), n)]
+            op("n", (s + str(t), n), "snd" + s + str(t), k)
         zq, zs = T["zq%d" % t], T["zs%d" % t]
         quant(zq[:, 0:320], zs[:, 0:320], T.zt[:], zk, "zqa%d" % t)
         for k in range(10 - VEC_COUNTS, 10):
             cp(v("hv"), v("pk", 320 * k, 320 * k + 320).indirect(v("rl")), "pk rl", "hv")
-            V(lambda: vec.tensor_reduce(v("hc", k, k + 1), v("hv"), AxisListType.X, OP.add), "hv", "hd")
+            red(v("hc", k, k + 1), v("hv"), OP.add, "hv", "hd", 320)
 
         tr(v("h1"), v("hc"), "hc" + (" hd" if VEC_COUNTS else ""), "h1")
         tt(v("h2"), v("h1", 0, 16), v("h1", 16, 32), OP.add, "h1", "h2")
@@ -483,17 +566,17 @@ def rank_program(g, core, T, topo):
         tr(v("nr", 32, 64), v("nr", 0, 32), "nr0", "nr1")
         ts(v("nr", 64, 96), v("nr", 32, 64), 64.0, None, OP.is_gt, None, "nr1", "nr2")
         ts(v("nr", 96, 128), v("nr", 32, 64), 64.0, FAR, OP.is_le, OP.mult, "nr1", "nr3")
-        V(lambda: vec.tensor_reduce(v("nv", 1, 2), v("nr", 64, 96), AxisListType.X, OP.add), "nr2", "nv1")
+        red(v("nv", 1, 2), v("nr", 64, 96), OP.add, "nr2", "nv1")
         tt(v("nr", 128, 160), v("nr", 96, 128), v("nr", 32, 64), OP.add, "nr3 nr1", "nr4")
         ts(v("nv", 3, 4), v("nv", 1, 2), -1.0, None, OP.add, None, "nv1", "nv3")
-        V(lambda: vec.tensor_reduce(v("nv", 2, 3), v("nr", 128, 160), AxisListType.X, OP.min), "nr4", "nv2")
+        red(v("nv", 2, 3), v("nr", 128, 160), OP.min, "nr4", "nv2")
         ts(v("ceq"), v("cf"), v("nv", 3, 4), None, OP.is_equal, None, "cf nv3", "ceq")
         ts(v("nv", 4, 5), v("nv", 2, 3), 0.5, -32.0, OP.mult, OP.add, "nv2", "nv4")
-        V(lambda: vec.tensor_tensor_scan(v("pe"), v("ceq"), v("zb", 0, 320), 0.0, OP.add, OP.max), "ceq zb", "pe")
+        scan(v("pe"), v("ceq"), v("zb", 0, 320), 0.0, "ceq zb", "pe")
         ts(v("cw"), v("pe"), v("nv", 4, 5), 0.5, OP.is_gt, OP.mult, "pe nv4", "cw")
         tt(v("cx"), v("cf"), v("cw"), OP.add, "cf cw", "cx")
         ts(v("gone"), v("cx"), v("nv", 3, 4), None, OP.is_le, None, "cx nv3", "gone")
-        V(lambda: vec.tensor_tensor_scan(v("pg"), v("gone"), v("zb", 0, 320), 319.0, OP.add, OP.max), "gone zb", "pg")
+        scan(v("pg"), v("gone"), v("zb", 0, 320), 319.0, "gone zb", "pg")
         ac(v("gn"), v("gone"), "gone", "gn", AF.Copy, scale=-FAR)
         tt(v("py"), v("pg"), v("gone"), OP.mult, "pg gone", "py")
         tt(T.sa[:, :, 0:16], v("py"), v("iof"), OP.max, "py iof", "sa0")
@@ -518,10 +601,10 @@ def rank_program(g, core, T, topo):
         nx = "xq%d" % (t + 1)
         nq, ns = T[nx], T["xs%d" % (t + 1)]
         zz = "zqa%d zqb%d sel%d" % (t, t, t)
-        V(lambda: vec.tensor_copy(nq[:].bitcast(dt.uint32), zq[:].bitcast(dt.uint32).indirect(sel)), zz, nx + "c")
-        op("a", lambda: act.activation(ns[:], zs[:].indirect(sel), AF.Copy), zz, nx + "s")
-        lw[nx] = lw[nx + "c"] + lw[nx + "s"]
+        cp(nq[:].bitcast(dt.uint32), zq[:].bitcast(dt.uint32).indirect(sel), zz, nx + "c", 320, 1.6)
+        ac(ns[:], zs[:].indirect(sel), zz, nx + "s", n=320, k=1.6)
         if t == R - 1:
+            nx = nx + "c " + nx + "s"
             mm(0, 320, (T.vq[:], T.vs[:]), (nq[:], ns[:]), "vq " + nx)
             store(T.oc[:], nq[:].bitcast(dt.uint8), nx)
             for k in range(4):
@@ -549,6 +632,9 @@ def rank_program(g, core, T, topo):
             ac(T.la[:, :, 0:16], v("lkf"), "lkf", "la0")
             ac(T.la[:, :, 16:32], v("lkf"), "lkf", "la1")
             new_links.append(t)
+    for i in schedule():
+        o = ops[i]
+        emit(o["q"], o["f"], o["r"], o["w"], o["dma"], o["fill"])
     for q in ("v", "a", "t", "g"):
         g.wait_ge(T.sem["s" + q], cnt[q])
     for i in range(ndma[0]):

@@ -8,28 +8,30 @@ NT = [max(128, 64 * (m + 1)) for m in range(5)]
 KEYS = ["KE0", "KE1", "KE2", "KE3", "KH0", "KH1", "KH2", "KH3", "Ge", "Go", "SDe", "SDo", "ODe", "ODo", "KB"]
 USEG = ["UB", "US", "USe", "USo", "UO", "UOe", "UOo"]
 EARLY = 10
-ACT_ORDER = (1, 2, 3, 4, 5)
-GATHER_AT = 3
-VEC_COUNTS = 1
+ACT_ORDER = (1, 2, 3, 4, 5, 6, 7, 8)
+GATHER_AT = 6
+VEC_COUNTS = 3
 
-APART = ["TB", "eq", "rss", "rso", "hc", "hd", "thx", "e4", "pk", "h4", "kg0", "kg1"] + ["TS%d" % _m for _m in range(5)] + ["TO%d" % _m for _m in range(5)] + ["ps%d" % _m for _m in range(8)]
+APART = ["TB", "eq", "rss", "rso", "hc", "hd", "yp", "h2", "e4", "pk", "h4", "kg0", "kg1"] + ["TS%d" % _m for _m in range(5)] + ["TO%d" % _m for _m in range(5)] + ["TP%d" % _m for _m in range(5)] + ["ps%d" % _m for _m in range(8)]
 
-CYCLE, WAKE = 0.00103, 0.1
+ON_ACT, ON_VEC = ["e1", "e2", "kg0", "kg1", "rt1", "rt3", "sa0"], ["dx", "ga0", "kb1"]
+CYCLE, WAKE = 0.0009, 0.2
 SIZE = {_k: 640 for _k in "lxs lxo tt ct cu st lt".split()}
 SIZE.update({_k: 64 for _k in ("p1 p2 p3 p4 sl nsl slo pls plo ru y4 y5 ri rj rl ti tj l3u e1 e2 ef e4 es0 es1 es2 h1 h2 h3a h3b h4 h4b h5 hi hj hk hm hn hw nr0 nr1 nr2 nr3 nr4 "
                               "nv1 nv2 nv3 nv4 sel0 sel1 sel2 l1 l2 l3 li lj L0 L1 L2 thx own own0 inm inb rss rso hc").split()})
 SIZE.update({"pf%d" % _k: 64 for _k in range(10)})
-SIZE.update({"v6": 120, "y1": 120, "ea0": 128, "ea1": 128, "et": 256, "lw1": 200, "pk": 64, "gm0": 128, "gm1": 128, "kg0": 128, "kg1": 128, "kt1": 128})
+SIZE.update({_k: 64 for _k in "plr plq yp ri pq gl sf nvt".split()})
+SIZE.update({"v6": 120, "va6": 120, "vb6": 120, "vw": 120, "yq": 120, "ys": 120, "rsm": 120, "wqt": 120, "ea0": 128, "ea1": 128, "et": 256, "lw1": 200, "pk": 64, "gm0": 128, "gm1": 128, "kg0": 128, "kg1": 128, "kt1": 128})
 
 F8 = "float8_e4m3fn_x4"
 ARENA = {
-    "fc": ("float32", [("pf", 16), ("iof", 320), ("ci", 320), ("cg", 256), ("ms", 320), ("mo", 320), ("m1", 320), ("inm", 16), ("b16", 20), ("one", 32)]),
+    "fc": ("float32", [("pf", 16), ("iof", 320), ("ci", 320), ("cg", 256), ("ms", 320), ("mo", 320), ("m1", 320), ("inm", 16), ("b16", 20), ("one", 32), ("wqt", 120), ("rsm", 120)]),
     "ic": ("int32", [("pii", 8), ("uli", 56), ("eli", 20), ("ioi", 320)]),
     "uc": ("uint16", [("ul", 56), ("el", 20)]),
     "bc": ("bfloat16", [("zb", 1280), ("bm", 320), ("pk", 3200), ("gmk", 384)]),
-    "fp": ("float32", [("sl", 20), ("nsl", 20), ("slo", 20), ("df0", 320), ("df1", 320), ("rss", 20), ("rso", 20)]),
-    "fl": ("float32", [("va", 320), ("inj", 1920), ("aw0", 320), ("aw1", 320), ("a6f", 320), ("dw", 320), ("dx", 320), ("dy", 320), ("y5", 20), ("hs0", 320), ("hs1", 320), ("hv", 320), ("hc", 32), ("h1", 32),
-                       ("h2", 16), ("h3", 16), ("h4", 32), ("h5", 32), ("hm", 16), ("hn", 16), ("hw", 16), ("nv", 16), ("nr", 160),
+    "fp": ("float32", [("sl", 20), ("nsl", 20), ("slo", 20), ("df0", 320), ("df1", 320), ("df2", 320), ("df3", 320), ("rss", 20), ("rso", 20)]),
+    "fl": ("float32", [("va", 320), ("inj", 1920), ("aw0", 320), ("aw1", 320), ("a6f", 320), ("dw", 320), ("dx", 320), ("plr", 20), ("plq", 20), ("va6", 120), ("vb6", 120), ("v6", 120), ("vw", 120), ("yp", 120), ("yq", 120), ("ys", 120), ("ck", 320), ("pq", 20), ("gl", 20), ("sf", 20), ("hs0", 320), ("hs1", 320), ("hv", 320), ("hc", 32), ("h1", 32),
+                       ("h2", 32), ("h3", 32), ("h4", 32), ("h5", 32), ("hm", 16), ("hn", 16), ("hw", 16), ("nv", 16), ("nr", 160),
                        ("pe", 320), ("pg", 320), ("py", 320), ("gn", 320), ("kb0", 320), ("kb1", 320), ("kb2", 320), ("kb3", 320),
                        ("pls", 20), ("plo", 20), ("er", 320), ("e1", 8), ("e2", 8), ("ef", 8), ("l1", 20), ("l2", 20), ("l3", 20), ("lkf", 320), ("lw", 448), ("own", 20)]),
     "il": ("int32", [("ri", 20), ("rj", 20), ("ti", 20), ("tj", 20), ("hi", 16), ("hj", 16), ("hk", 16), ("fi", 320), ("fj", 320), ("li", 20), ("lj", 20)]),
@@ -47,9 +49,10 @@ for _a, (_d, _l) in ARENA.items():
     SCRATCH[_a] = ("sbuf", [128, _o], _d)
 for _n, _w in (("xt", 1280), ("ut", 512), ("vt", 512), ("kt", 4112), ("TB", 1280), ("eq", 320), ("TS", 6400), ("TO", 6400), ("TD", 1280), ("fw", 1280), ("zt", 1280), ("ett", 512), ("rt", 512)):
     SCRATCH[_n] = ("sbuf", [128, _w], "bfloat16")
-for _n, _w in (("alt", 32), ("lxs", 32), ("lxo", 32), ("ca", 32), ("cb", 32), ("ct", 32), ("cu", 32), ("a6", 32), ("tt", 32), ("sa", 32), ("st", 32), ("la", 32), ("lt", 32),
-               ("v6", 6), ("thx", 6), ("y1", 6), ("wqt", 6), ("y4", 3)):
+for _n, _w in (("alt", 32), ("lxs", 32), ("lxo", 32), ("ca", 32), ("cb", 32), ("ct", 32), ("cu", 32), ("a6", 32), ("tt", 32), ("sa", 32), ("st", 32), ("la", 32), ("lt", 32)):
     SCRATCH[_n] = ("sbuf", [128, 20, _w], "float32")
+SCRATCH["ga"] = ("sbuf", [128, 20, 32], "bfloat16")
+SCRATCH["gt"] = ("sbuf", [128, 20, 32], "bfloat16")
 SCRATCH["ea"] = ("sbuf", [128, 8, 32], "float32")
 SCRATCH["et"] = ("sbuf", [128, 8, 32], "float32")
 SCRATCH["olt"] = ("sbuf", [128, 20], "int32")
@@ -203,15 +206,24 @@ def rank_program(g, core, T, topo):
         b = n if b is None else b
         return T[ar][:, o + a:o + b] if p is None else T[ar][p[0]:p[1], o + a:o + b]
 
+    def every(name, a, step):
+        ar, o, n = POS[name]
+        return T[ar][:, o + a:o + n:step]
+
     def V(f, r, w, n=0, k=1.0):
         n = n or SIZE.get(w.split()[0], 320)
         op("v", f, r, w, c=CYCLE * max(64.0, n * k))
 
     def cp(out, in_, r, w, n=0, k=1.0):
-        V(lambda: vec.tensor_copy(out, in_), r, w, n, k)
+        if w in ON_ACT:
+            ac(out, in_, r, w, n=n, k=k)
+        else:
+            V(lambda: vec.tensor_copy(out, in_), r, w, n, k)
 
     def ts(out, a, s1, s2, o1, o2, r, w, n=0):
-        if o2 is None:
+        if w in ON_ACT:
+            ac(out, a, r, w, n=n, scale=s1)
+        elif o2 is None:
             V(lambda: vec.tensor_scalar(out, a, s1, None, o1), r, w, n)
         else:
             V(lambda: vec.tensor_scalar(out, a, s1, s2, o1, o2), r, w, n)
@@ -231,8 +243,16 @@ def rank_program(g, core, T, topo):
     def fill(ap, c, w, n=0):
         op("v", lambda: vec.memset(ap, c), "", w, c=CYCLE * max(64.0, 0.5 * (n or SIZE.get(w, 320))), fill=True)
 
-    def ac(out, in_, r, w, func=AF.Copy, n=0, k=1.0, **kw):
-        op("a", lambda: act.activation(out, in_, func, **kw), r, w, c=CYCLE * max(64.0, k * (n or SIZE.get(w.split()[0], 320))))
+    def ac(out, in_, r, w, func=AF.Copy, n=0, k=1.0, fill=False, **kw):
+        if w in ON_VEC:
+            if "bias" in kw:
+                ts(out, in_, kw["bias"], None, OP.add, None, r, w, n)
+            elif "scale" in kw:
+                ts(out, in_, kw["scale"], None, OP.mult, None, r, w, n)
+            else:
+                cp(out, in_, r, w, n, k)
+            return
+        op("a", lambda: act.activation(out, in_, func, **kw), r, w, c=CYCLE * max(64.0, k * (n or SIZE.get(w.split()[0], 320))) + (0.02 if "accum_out" in kw else 0.0), fill=fill)
 
     def quant(q, s, t_, r, w, n=320):
         op("v", lambda: vec.quantize_mx(q, s, t_), r, w, c=0.015 + 0.0011 * n)
@@ -240,8 +260,11 @@ def rank_program(g, core, T, topo):
     def mm(bank, n, L, M, r, start=True, stop=True):
         op("t", lambda: g.tensor.matmul_mx(T["ps%d" % bank][:, 0:n], L[0], L[1], M[0], M[1], start, stop), r, "ps%d" % bank, c=1.5 * CYCLE * (n + 16))
 
-    def iota(ap, pat, first, w, fl=False, cm=0):
-        op("g", lambda: g.iota(ap, pat, first, cm, **({"allow_small_or_imprecise_dtypes": True} if fl else {})), "", w, c=0.3)
+    def zeros(ap, n, w):
+        ac(ap, v("zb", 0, n), "zb", w, n=n, fill=True)
+
+    def iota(ap, pat, first, w, fl=False, cm=0, c=0.3, fill=False):
+        op("g", lambda: g.iota(ap, pat, first, cm, **({"allow_small_or_imprecise_dtypes": True} if fl else {})), "", w, c=c, fill=fill)
 
     def load(dst, src, w):
         op("s", lambda: g.sync.dma_start(dst, src), "", w, dma=True, c=0.1)
@@ -263,7 +286,7 @@ def rank_program(g, core, T, topo):
 
     def pcol(i):
         return v("pf", i, i + 1)
-    Q16, P32, PAR, ME, MO, PG, PF, BE, BO, TBI = range(10)
+    Q16, P32, PAR, ME, MO, PG, PF, BE, BO, TBI, HSC, HOF = range(12)
 
     load(T.ut[:], T.u[:], "ut")
     load(T.xt[:], T.x[:], "xt")
@@ -280,7 +303,7 @@ def rank_program(g, core, T, topo):
     iota(v("cg", 128, 256), [[2, 4], [0, 32]], 1, "cg", True)
     iota(v("inm", 0, 6), [[-1, 6]], 6, "inm", True)
     iota(v("b16"), [[16, 20]], 0, "b16", True)
-    iota(T.wqt[:], [[0, 20], [-1, 6]], 6, "wqt", True)
+    iota(v("wqt"), [[0, 20], [-1, 6]], 6, "wqt", True)
     iota(v("eli"), [[1, 10], [0, 2]], 0, "eli")
 
     fill(v("zb"), 0.0, "zb")
@@ -305,16 +328,17 @@ def rank_program(g, core, T, topo):
     quant(T.xq0[:], T.xs0[:], T.xt[:], "xt", "xq0c xq0s")
     ts(v("m1"), v("ci"), pcol(Q16), pcol(BO), OP.is_le, OP.mult, "ci pf0 pf8", "m1")
     tt(v("ms"), v("ms"), v("m1"), OP.add, "ms m1", "ms")
-    fill(T.TB[:], 0.0, "TB")
+    zeros(T.TB[:], 1280, "TB")
     fill(T.eq[:], 0.0, "eq")
     for m in range(4, -1, -1):
-        ac(T.TS[:, 1280 * m:1280 * m + 4 * NT[m]], v("zb", 0, 4 * NT[m]), "zb", "TS%d" % m)
+        ac(T.TS[:, 1280 * m:1280 * m + 4 * NT[m]], v("zb", 0, 4 * NT[m]), "zb", "TS%d" % m, n=4 * NT[m], fill=True)
 
     def consts_births():
         fill(T.kt[:, 0:512], 512.0, "kt0")
         quant(*kst("KB"), T.kt[:, 0:512], "kt0", "kB")
-        fill(T.kt[:, 512:2064], 0.0, "kt1")
-        fill(T.kt[:, 3088:3604], 0.0, "kt2")
+        zeros(T.kt[:, 512:1536], 1024, "kt1")
+        zeros(T.kt[:, 1536:2064], 528, "kt1")
+        zeros(T.kt[:, 3088:3604], 516, "kt2")
         ts(T.kt[:, 3091:3603:4], v("iof", 0, 128), pcol(PF), 0.5, OP.is_equal, OP.mult, "iof pf6", "kt2")
         ts(T.kt[:, 515:1027:4], v("iof", 0, 128), pcol(PF), 128.0, OP.is_equal, OP.mult, "iof pf6", "kt1")
         for b in range(4):
@@ -323,7 +347,7 @@ def rank_program(g, core, T, topo):
 
     def consts_order():
         for m in range(4, -1, -1):
-            fill(T.TO[:, 1280 * m:1280 * m + 4 * NT[m]], 0.0, "TO%d" % m)
+            iota(T.TO[:, 1280 * m:1280 * m + 4 * NT[m]], [[0, 4 * NT[m]]], 0, "TO%d TP%d" % (m, m), True, c=0.13 + 8 * NT[m] * CYCLE, fill=True)
         ts(v("inm", 0, 6), v("inm", 0, 6), pcol(Q16), None, OP.is_equal, None, "inm pf0", "inm")
         ts(v("inm", 8, 14), v("inm", 0, 6), -1.0, None, OP.add, None, "inm", "inb")
 
@@ -342,13 +366,17 @@ def rank_program(g, core, T, topo):
         cp(v("lst0"), T.olt[:], "olt", "L0")
         ts(v("own"), v("own"), pcol(Q16), None, OP.add, None, "own0 pf0", "own0")
         tt(v("own"), v("b16"), v("own"), OP.add, "b16 own0", "own")
-        ts(T.wqt[:], T.wqt[:], 262144.0, None, OP.mult, None, "wqt", "wqt")
-        fill(T.thx[:], FAR, "thx")
+        ts(v("rsm"), v("wqt"), 6.0, None, OP.is_lt, None, "wqt", "rsm")
+        ts(v("wqt"), v("wqt"), 262144.0, None, OP.mult, None, "wqt", "wqt")
+        fill(v("yp"), 1.0, "yp")
         ts(v("bm"), v("ci"), pcol(Q16), None, OP.is_equal, None, "ci pf0", "bm")
-        fill(v("pk"), 0.0, "pk")
+        for o in (0, 1280, 2560):
+            zeros(v("pk", o, min(o + 1280, 3200)), min(1280, 3200 - o), "pk")
 
     def consts_counts():
-        ts(pcol(TBI), pcol(P32), -1.0, 0.5, OP.mult, OP.add, "pf1", "pf9")
+        ts(pcol(TBI), pcol(P32), -1.0, -0.5, OP.mult, OP.add, "pf1", "pf9")
+        ts(pcol(HSC), pcol(MO), 1.0 / 4096 - 1.0, 1.0, OP.mult, OP.add, "pf4", "pf10")
+        ts(pcol(HOF), pcol(MO), -0.3125, None, OP.mult, None, "pf4", "pf11")
         cp(v("el"), v("eli"), "eli", "el")
         fill(v("hc"), 0.0, "hc")
         fill(v("hw"), 0.0, "hw")
@@ -391,9 +419,9 @@ def rank_program(g, core, T, topo):
 
         def snapshots(ms_):
             for m in ms_:
-                n, o, d = 16 * m, 1280 * (m // 4) + m % 4, "df%d" % (m % 2)
-                ac(v(d, 0, n), ps(6, n), "ps6 nsl", d, AF.Relu, bias=v("nsl", m, m + 1))
-                ac(T.TS[:, o:o + 4 * n:4], v(d, 0, n), d, "TS%d rss" % (m // 4), AF.Sign, accum_out=v("rss", m, m + 1))
+                n, o, d = 16 * m, 1280 * (m // 4) + m % 4, "df%d" % (m % 4)
+                ac(v(d, 0, n), ps(6, n), "ps6 nsl", d, AF.Relu, bias=v("nsl", m, m + 1), n=n)
+                ac(T.TS[:, o:o + 4 * n:4], v(d, 0, n), d, "TS%d rss" % (m // 4), AF.Sign, accum_out=v("rss", m, m + 1), n=n)
         snapshots(range(19, EARLY - 1, -1))
         if new_links:
             lists_of_links(new_links.pop())
@@ -433,20 +461,20 @@ def rank_program(g, core, T, topo):
         for m in range(19, 0, -1):
             if m not in ACT_ORDER:
                 n, o = 16 * m, 1280 * (m // 4) + m % 4
-                ts(T.TO[:, o:o + 4 * n:4], ps(7, n), v("slo", m, m + 1), None, OP.is_lt, None, "ps7 slo", "TO%d o%d" % (m // 4, m))
+                ts(T.TO[:, o:o + 4 * n:4], ps(7, n), v("slo", m, m + 1), None, OP.is_lt, None, "ps7 slo", "TO%d o%d" % (m // 4, m), n)
         if t == 0:
             consts_reading()
         quant(T.dq[:], T.ds[:], T.TD[:], "TD0 TD1 TD2 TD3", "dq")
         for m in range(19, 0, -1):
-            n, o, d = 16 * m, 1280 * (m // 4) + m % 4, "df%d" % (m % 2)
+            n, o, d = 16 * m, 1280 * (m // 4) + m % 4, "df%d" % (m % 4)
             if m in ACT_ORDER:
-                ac(v(d, 0, n), ps(5, n), "ps5 slo", d, AF.Relu, bias=v("slo", m, m + 1), scale=-1.0)
-                ac(T.TO[:, o:o + 4 * n:4], v(d, 0, n), d, "TO%d rso" % (m // 4), AF.Sign, accum_out=v("rso", m, m + 1))
+                ac(v(d, 0, n), ps(5, n), "ps5 slo", d, AF.Relu, bias=v("slo", m, m + 1), scale=-1.0, n=n)
+                ac(T.TO[:, o:o + 4 * n:4], v(d, 0, n), d, "TP%d rso" % (m // 4), AF.Sign, accum_out=v("rso", m, m + 1), n=n)
         for m in range(19, 0, -1):
             n, o = 16 * m, 1280 * (m // 4) + m % 4
             if m not in ACT_ORDER:
                 d = "dump%d" % (m % 2)
-                ac(v(d, 0, n), T.TO[:, o:o + 4 * n:4], "o%d" % m, d + " rso", AF.Copy, accum_out=v("rso", m, m + 1))
+                ac(v(d, 0, n), T.TO[:, o:o + 4 * n:4], "o%d" % m, d + " rso", AF.Copy, accum_out=v("rso", m, m + 1), n=n)
         if t == 0:
             consts_counts()
             for k in range(10):
@@ -468,36 +496,35 @@ def rank_program(g, core, T, topo):
                 mm(banks[i], 320, kst(pre + n), (T.dq[:], T.ds[:]), "k%s%s dq" % (pre[0], n), True, False)
             for m in range(4, -1, -1):
                 p = pair(q, s, 320 * m, NT[m])
-                quant(p[0], p[1], T[tile][:, 1280 * m:1280 * m + 4 * NT[m]], "%s%d" % (key, m), "q%s%d" % (key, m))
+                quant(p[0], p[1], T[tile][:, 1280 * m:1280 * m + 4 * NT[m]], key % ((m,) * key.count("%")), "q%s%d" % (tile, m), NT[m])
                 for i, n in enumerate("eo"):
-                    mm(banks[i], NT[m], kst("G" + n), p, "kG%s q%s%d" % (n, key, m), False, m == 0)
+                    mm(banks[i], NT[m], kst("G" + n), p, "kG%s q%s%d" % (n, tile, m), False, m == 0)
 
-        sums("TS", "sq", "ss", "TS", (4, 6), "SD")
-        sums("TO", "oq", "osq", "TO", (5, 7), "OD")
-        tt(v("pls"), v("b16"), v("rss"), OP.subtract, "b16 rss", "pls")
+        sums("TS", "sq", "ss", "TS%d", (4, 6), "SD")
+        sums("TO", "oq", "osq", "TO%d TP%d", (5, 7), "OD")
+        tt(v("plr"), v("b16"), v("rss"), OP.subtract, "b16 rss", "plr")
+        ts(v("plq"), v("plr"), 512.0, 512.0, OP.mult, OP.add, "plr", "plq")
         tr(T.tt[:], T.a6[:], "a60 a61", "tt")
-        ts(T.v6[:], T.tt[:, :, 1:7], pcol(ME), None, OP.mult, None, "tt pf3", "v6")
-        ts(T.y1[:], T.tt[:, :, 17:23], pcol(MO), None, OP.mult, None, "tt pf4", "y1")
-        tt(T.v6[:], T.v6[:], T.y1[:], OP.add, "v6 y1", "v6")
-        cp(v("ti"), T.v6[:, :, 2], "v6", "ti")
+        ts(v("va6"), T.tt[:, :, 1:7], pcol(ME), None, OP.mult, None, "tt pf3", "va6")
+        ts(v("vb6"), T.tt[:, :, 17:23], pcol(MO), None, OP.mult, None, "tt pf4", "vb6")
+        tt(v("v6"), v("va6"), v("vb6"), OP.add, "va6 vb6", "v6")
+        tt(v("vw"), v("v6"), v("wqt"), OP.add, "v6 wqt", "vw")
+        cp(v("ti"), every("v6", 2, 6), "v6", "ti")
         ts(v("tj"), v("ti"), 511, None, OP.bitwise_and, None, "ti", "tj")
         cp(v("l3u"), v("tj"), "tj", "l3u")
-        ac(T.cb[:, :, 0:16], ps(4), "ps4", "cb0")
-        ac(T.cb[:, :, 16:32], ps(6), "ps6", "cb1")
+        ac(T.cb[:, :, 0:16], ps(4), "ps4", "cb0", scale=512.0)
+        ts(T.cb[:, :, 16:32], ps(6), 512.0, None, OP.mult, None, "ps6", "cb1")
         tr(T.cu[:], T.cb[:], "cb0 cb1", "cu")
-        tt(v("pls"), v("pls"), T.cu[:, :, 0], OP.add, "pls cu", "pls")
+        tt(v("pls"), v("plq"), T.cu[:, :, 0], OP.add, "plq cu", "pls")
         for i in range(5):
-            ac(T.thx[:, :, i], v("pls"), "pls", "thx", AF.Copy, scale=512.0, bias=512.0)
-        tt(T.y1[:], T.v6[:], T.thx[:], OP.is_lt, "v6 thx", "y1")
-        tt(T.y1[:], T.y1[:], T.wqt[:], OP.mult, "y1 wqt", "y1")
-        tt(T.y1[:], T.y1[:], T.v6[:], OP.add, "y1 v6", "y1")
-        tt(T.y4[:], T.y1[:, :, 0:3], T.y1[:, :, 3:6], OP.max, "y1", "y4")
-        tt(v("y5"), T.y4[:, :, 0], T.y4[:, :, 1], OP.max, "y4", "y5")
-        tt(v("ri"), v("y5"), T.y4[:, :, 2], OP.max, "y5 y4", "ri")
+            tt(every("yp", i, 6), every("v6", i, 6), v("pls"), OP.is_lt, "v6 pls", "yp")
+        tt(v("yq"), v("yp"), v("vw"), OP.mult, "yp vw", "yq")
+        V(lambda: vec.tensor_tensor_scan(v("ys"), v("rsm"), v("yq"), 0.0, OP.mult, OP.max), "yq rsm", "ys")
+        cp(v("ri"), every("ys", 5, 6), "ys", "ri")
         ts(v("rj"), v("ri"), 511, None, OP.bitwise_and, None, "ri", "rj")
         cp(v("rl"), v("rj"), "rj", "rl")
         for k in range(10 - VEC_COUNTS):
-            if k == GATHER_AT:
+            if k == min(GATHER_AT, 9 - VEC_COUNTS):
                 for b in range(4):
                     ac(v("zg%d" % b), T.fw[:, 320 * b:320 * b + 320].indirect(v("rl")), "fw%d rl" % b, "zg%d" % b)
             d = "hs%d" % (k % 2)
@@ -546,19 +573,16 @@ def rank_program(g, core, T, topo):
             red(v("hc", k, k + 1), v("hv"), OP.add, "hv", "hd", 320)
 
         tr(v("h1"), v("hc"), "hc" + (" hd" if VEC_COUNTS else ""), "h1")
-        tt(v("h2"), v("h1", 0, 16), v("h1", 16, 32), OP.add, "h1", "h2")
-        tt(v("h3", 0, 16, (0, 32)), v("h2", 0, 16, (0, 32)), v("h2", 0, 16, (32, 64)), OP.add, "h2", "h3a")
-        tt(v("h3", 0, 16, (64, 96)), v("h2", 0, 16, (64, 96)), v("h2", 0, 16, (96, 128)), OP.add, "h2", "h3b")
+        for a in (0, 16):
+            tt(v("h2", a, a + 16), v("h1", 0, 16), v("h1", 16, 32), OP.add, "h1", "h2")
+        tt(v("h3", 0, 32, (0, 32)), v("h2", 0, 32, (0, 32)), v("h2", 0, 32, (32, 64)), OP.add, "h2", "h3a")
+        tt(v("h3", 0, 32, (64, 96)), v("h2", 0, 32, (64, 96)), v("h2", 0, 32, (96, 128)), OP.add, "h2", "h3b")
         for a in range(4):
-            tt(v("h4", 0, 16, (32 * a, 32 * a + 32)), v("h3", 0, 16, (0, 32)), v("h3", 0, 16, (64, 96)), OP.add, "h3a h3b", "h4")
-        cp(v("h4", 16, 32), v("h4", 0, 16), "h4", "h4b")
-        tr(v("h5"), v("h4"), "h4 h4b", "h5")
-        cp(v("hi", 0, 10), v("h5", 0, 10), "h5", "hi")
+            tt(v("h4", 0, 32, (32 * a, 32 * a + 32)), v("h3", 0, 32, (0, 32)), v("h3", 0, 32, (64, 96)), OP.add, "h3a h3b", "h4")
+        tr(v("h5"), v("h4"), "h4", "h5")
+        ts(v("hi", 0, 10), v("h5", 0, 10), pcol(HSC), pcol(HOF), OP.mult, OP.add, "h5 pf10 pf11", "hi")
         ts(v("hj", 0, 10), v("hi", 0, 10), 4095, None, OP.bitwise_and, None, "hi", "hj")
-        ts(v("hk", 0, 10), v("hi", 0, 10), 12, None, OP.logical_shift_right, None, "hi", "hk")
-        ts(v("hm", 0, 10), v("hj", 0, 10), pcol(ME), 64.0, OP.mult, OP.min, "hj pf3", "hm")
-        ts(v("hn", 0, 10), v("hk", 0, 10), pcol(MO), 64.0, OP.mult, OP.min, "hk pf4", "hn")
-        tt(v("hw", 0, 10), v("hm", 0, 10), v("hn", 0, 10), OP.add, "hm hn", "hw")
+        ts(v("hw", 0, 10), v("hj", 0, 10), 63.0, 1.0, OP.min, OP.add, "hj", "hw")
         ac(v("hx"), v("hw").indirect(v("el")), "hw el", "hx")
         tr(v("cf"), v("hx"), "hx", "cf")
         ac(v("dump0"), v("cf"), "cf pf9", "dump0 nv0", AF.Sign, bias=pcol(TBI), accum_out=v("nv", 0, 1))
@@ -568,23 +592,27 @@ def rank_program(g, core, T, topo):
         ts(v("nr", 96, 128), v("nr", 32, 64), 64.0, FAR, OP.is_le, OP.mult, "nr1", "nr3")
         red(v("nv", 1, 2), v("nr", 64, 96), OP.add, "nr2", "nv1")
         tt(v("nr", 128, 160), v("nr", 96, 128), v("nr", 32, 64), OP.add, "nr3 nr1", "nr4")
-        ts(v("nv", 3, 4), v("nv", 1, 2), -1.0, None, OP.add, None, "nv1", "nv3")
         red(v("nv", 2, 3), v("nr", 128, 160), OP.min, "nr4", "nv2")
-        ts(v("ceq"), v("cf"), v("nv", 3, 4), None, OP.is_equal, None, "cf nv3", "ceq")
-        ts(v("nv", 4, 5), v("nv", 2, 3), 0.5, -32.0, OP.mult, OP.add, "nv2", "nv4")
-        scan(v("pe"), v("ceq"), v("zb", 0, 320), 0.0, "ceq zb", "pe")
-        ts(v("cw"), v("pe"), v("nv", 4, 5), 0.5, OP.is_gt, OP.mult, "pe nv4", "cw")
-        tt(v("cx"), v("cf"), v("cw"), OP.add, "cf cw", "cx")
-        ts(v("gone"), v("cx"), v("nv", 3, 4), None, OP.is_le, None, "cx nv3", "gone")
+        ts(v("ceq"), v("cf"), v("nv", 1, 2), 2.0, OP.is_equal, OP.mult, "cf nv1", "ceq")
+        ts(v("nv", 3, 4), v("nv", 1, 2), 1024.0, None, OP.mult, None, "nv1", "nv3")
+        tt(v("nv", 4, 5), v("nv", 3, 4), v("nv", 2, 3), OP.add, "nv3 nv2", "nv4")
+        ac(v("ck"), v("cf"), "cf", "ck", scale=1024.0)
+        scan(v("pe"), v("ceq"), v("zb", 0, 320), 64.0, "ceq zb", "pe")
+        tt(v("py"), v("pe"), v("ck"), OP.add, "pe ck", "py")
+        ts(v("gone"), v("py"), v("nv", 4, 5), None, OP.is_le, None, "py nv4", "gone")
         scan(v("pg"), v("gone"), v("zb", 0, 320), 319.0, "gone zb", "pg")
+        ac(T.ga[:, :, 0:16], v("gone"), "gone", "ga0")
+        ac(T.ga[:, :, 16:32], v("gone"), "gone", "ga1")
         ac(v("gn"), v("gone"), "gone", "gn", AF.Copy, scale=-FAR)
-        tt(v("py"), v("pg"), v("gone"), OP.mult, "pg gone", "py")
-        tt(T.sa[:, :, 0:16], v("py"), v("iof"), OP.max, "py iof", "sa0")
-        ac(T.sa[:, :, 16:32], T.sa[:, :, 0:16], "sa0", "sa1")
-        tt(v("kb0"), v("gn"), v("iof"), OP.add, "gn iof", "kb0")
+        cp(T.sa[:, :, 0:16], v("pg"), "pg", "sa0")
+        ac(T.sa[:, :, 16:32], v("pg"), "pg", "sa1")
+        tr(T.gt[:], T.ga[:], "ga0 ga1", "gt")
         tr(T.st[:], T.sa[:], "sa0 sa1", "st")
+        tt(v("pq"), T.st[:, :, 0], T.gt[:, :, 0], OP.mult, "st gt", "pq")
+        tt(v("sf"), v("pq"), v("own"), OP.max, "pq own", "sf")
         sel = v("sel%d" % t)
-        cp(sel, T.st[:, :, 0], "st", "sel%d" % t)
+        cp(sel, v("sf"), "sf", "sel%d" % t)
+        tt(v("kb0"), v("gn"), v("iof"), OP.add, "gn iof", "kb0")
 
         AQ = pair("aq%d" % t, "ap%d" % t, 0, 128)
         ak = "aq%d ap%d " % (t, t)

from concourse.mybir import dt, AluOpType, AxisListType, ActivationFunctionType

C, K, R, H = 320, 128, 3, 6
BIG = 1.0e29
FAR = 1.0e6
NSEM = 24
NT = [max(128, 64 * (m + 1)) for m in range(5)]
KEYS = ["KE0", "KE1", "KE2", "KE3", "KH0", "KH1", "KH2", "KH3", "Ge", "Go", "SDe", "SDo", "ODe", "ODo", "KB"]
USEG = ["UB", "US", "USe", "USo", "UO", "UOe", "UOo"]
EARLY = 10
ACT_ORDER = (1, 2, 3, 4, 5, 6, 7, 8)
GATHER_AT = 6
VEC_COUNTS = 3

APART = ["TB", "eq", "rss", "rso", "hc", "hd", "yp", "h2", "e4", "pk", "h4", "kg0", "kg1"] + ["TS%d" % _m for _m in range(5)] + ["TO%d" % _m for _m in range(5)] + ["TP%d" % _m for _m in range(5)] + ["ps%d" % _m for _m in range(8)]

ON_ACT, ON_VEC = ["e1", "e2", "kg0", "kg1", "rt1", "rt3", "sa0"], ["dx", "ga0", "kb1"]
CYCLE, WAKE = 0.0009, 0.2
SIZE = {_k: 640 for _k in "lxs lxo tt ct cu st lt".split()}
SIZE.update({_k: 64 for _k in ("p1 p2 p3 p4 sl nsl slo pls plo ru y4 y5 ri rj rl ti tj l3u e1 e2 ef e4 es0 es1 es2 h1 h2 h3a h3b h4 h4b h5 hi hj hk hm hn hw nr0 nr1 nr2 nr3 nr4 "
                              "nv1 nv2 nv3 nv4 sel0 sel1 sel2 l1 l2 l3 li lj L0 L1 L2 thx own own0 inm inb rss rso hc").split()})
SIZE.update({"pf%d" % _k: 64 for _k in range(10)})
SIZE.update({_k: 64 for _k in "plr plq yp ri pq gl sf nvt".split()})
SIZE.update({"v6": 120, "va6": 120, "vb6": 120, "vw": 120, "yq": 120, "ys": 120, "rsm": 120, "wqt": 120, "ea0": 128, "ea1": 128, "et": 256, "lw1": 200, "pk": 64, "gm0": 128, "gm1": 128, "kg0": 128, "kg1": 128, "kt1": 128})

F8 = "float8_e4m3fn_x4"
ARENA = {
    "fc": ("float32", [("pf", 16), ("iof", 320), ("ci", 320), ("cg", 256), ("ms", 320), ("mo", 320), ("m1", 320), ("inm", 16), ("b16", 20), ("one", 32), ("wqt", 120), ("rsm", 120)]),
    "ic": ("int32", [("pii", 8), ("uli", 56), ("eli", 20), ("ioi", 320)]),
    "uc": ("uint16", [("ul", 56), ("el", 20)]),
    "bc": ("bfloat16", [("zb", 1280), ("bm", 320), ("pk", 3200), ("gmk", 384)]),
    "fp": ("float32", [("sl", 20), ("nsl", 20), ("slo", 20), ("df0", 320), ("df1", 320), ("df2", 320), ("df3", 320), ("rss", 20), ("rso", 20)]),
    "fl": ("float32", [("va", 320), ("inj", 1920), ("aw0", 320), ("aw1", 320), ("a6f", 320), ("dw", 320), ("dx", 320), ("plr", 20), ("plq", 20), ("va6", 120), ("vb6", 120), ("v6", 120), ("vw", 120), ("yp", 120), ("yq", 120), ("ys", 120), ("ck", 320), ("pq", 20), ("gl", 20), ("sf", 20), ("hs0", 320), ("hs1", 320), ("hv", 320), ("hc", 32), ("h1", 32),
                       ("h2", 32), ("h3", 32), ("h4", 32), ("h5", 32), ("hm", 16), ("hn", 16), ("hw", 16), ("nv", 16), ("nr", 160),
                       ("pe", 320), ("pg", 320), ("py", 320), ("gn", 320), ("kb0", 320), ("kb1", 320), ("kb2", 320), ("kb3", 320),
                       ("pls", 20), ("plo", 20), ("er", 320), ("e1", 8), ("e2", 8), ("ef", 8), ("l1", 20), ("l2", 20), ("l3", 20), ("lkf", 320), ("lw", 448), ("own", 20)]),
    "il": ("int32", [("ri", 20), ("rj", 20), ("ti", 20), ("tj", 20), ("hi", 16), ("hj", 16), ("hk", 16), ("fi", 320), ("fj", 320), ("li", 20), ("lj", 20)]),
    "bz": ("bfloat16", [("zg0", 320), ("zg1", 320), ("zg2", 320), ("zg3", 320)]),
    "uo": ("uint16", [("rl", 20), ("ru", 20), ("e4", 32), ("l3u", 20), ("es0", 8), ("es1", 8), ("es2", 8), ("sel0", 20), ("sel1", 20), ("sel2", 20),
                      ("lst0", 20), ("lst1", 20), ("lst2", 20)]),
    "bl": ("bfloat16", [("dump0", 320), ("dump1", 320), ("hx", 320), ("cf", 320), ("ceq", 320), ("cw", 320), ("cx", 320), ("gone", 320)]),
}
POS, SCRATCH = {}, {}
for _a, (_d, _l) in ARENA.items():
    _o = 0
    for _n, _w in _l:
        POS[_n] = (_a, _o, _w)
        _o += (_w + 15) // 16 * 16
    SCRATCH[_a] = ("sbuf", [128, _o], _d)
for _n, _w in (("xt", 1280), ("ut", 512), ("vt", 512), ("kt", 4112), ("TB", 1280), ("eq", 320), ("TS", 6400), ("TO", 6400), ("TD", 1280), ("fw", 1280), ("zt", 1280), ("ett", 512), ("rt", 512)):
    SCRATCH[_n] = ("sbuf", [128, _w], "bfloat16")
for _n, _w in (("alt", 32), ("lxs", 32), ("lxo", 32), ("ca", 32), ("cb", 32), ("ct", 32), ("cu", 32), ("a6", 32), ("tt", 32), ("sa", 32), ("st", 32), ("la", 32), ("lt", 32)):
    SCRATCH[_n] = ("sbuf", [128, 20, _w], "float32")
SCRATCH["ga"] = ("sbuf", [128, 20, 32], "bfloat16")
SCRATCH["gt"] = ("sbuf", [128, 20, 32], "bfloat16")
SCRATCH["ea"] = ("sbuf", [128, 8, 32], "float32")
SCRATCH["et"] = ("sbuf", [128, 8, 32], "float32")
SCRATCH["olt"] = ("sbuf", [128, 20], "int32")
for _q, _s, _w in [("uq", "us", 128), ("vq", "vs", 128), ("upq", "ups", 896), ("wq", "wsp", 512), ("kq", "ks", 1920), ("bq", "bs", 320), ("sq", "ss", 1600), ("oq", "osq", 1600), ("dq", "ds", 320)] \
        + [("xq%d" % _t, "xs%d" % _t, 320) for _t in range(R + 1)] + [("zq%d" % _t, "zs%d" % _t, 448) for _t in range(R)] \
        + [("hq%d" % _t, "hp%d" % _t, 128) for _t in range(R)] + [("aq%d" % _t, "ap%d" % _t, 128) for _t in range(R)]:
    SCRATCH[_q] = ("sbuf", [128, _w], F8)
    SCRATCH[_s] = ("sbuf", [128, _w], "uint8")
for _t in range(R):
    SCRATCH["eland%d" % _t] = ("sbuf", [128, 8], "uint16")
for _b in range(8):
    SCRATCH["ps%d" % _b] = ("psum", [128, 512], "float32")
SEMAPHORES = ["sv", "sa", "st", "sg", "rloc"] + ["d%d" % i for i in range(NSEM)] + ["%s%d" % (k, t) for k in ("lA", "cA", "pA") for t in range(R)]


def rank_program(g, core, T, topo):
    rank = T.rank_of(core)
    if rank is None:
        return
    nxt = T.cores[(rank + 1) % len(T.cores)]
    prv = T.cores[(rank - 1) % len(T.cores)]
    OP, AF = AluOpType, ActivationFunctionType
    Q = {"v": g.vector, "a": g.scalar, "t": g.tensor, "g": g, "s": g.sync}
    cnt = {"v": 0, "a": 0, "t": 0, "g": 0}
    know = {q: {} for q in Q}
    snap, lw, rd, acc, filled, ndma = {}, {}, {}, {}, {}, [0]

    def wait(q, toks):
        need = {}
        for s, v_ in toks:
            if know[q].get(s, 0) < v_:
                need[s] = max(need.get(s, 0), v_)
        for s in list(need):
            for s2, v2 in need.items():
                if s2 != s and v2 and snap.get((s2, v2), {}).get(s, 0) >= need[s]:
                    need[s] = 0
                    break
        for s, v_ in need.items():
            if v_:
                Q[q].wait_ge(T.sem[s], v_)
                know[q][s] = v_
                for a, b in snap.get((s, v_), {}).items():
                    know[q][a] = max(know[q].get(a, 0), b)

    ops = []

    def op(q, f, r="", w="", dma=False, c=0, fill=False):
        ops.append({"q": q, "f": f, "r": r.split(), "w": w.split(), "dma": dma, "c": c, "fill": fill, "lat": 2.0 if dma else 2.6 if q == "n" else 0.0})

    def schedule():
        n = len(ops)
        pred = [{} for _ in ops]
        last, reads, bank = {}, {}, {}
        for i, o in enumerate(ops):
            p = pred[i]

            def dep(j, full=True):
                if j != i:
                    p[j] = p.get(j, False) or full
            for k in o["r"] + o["w"]:
                if k[:2] == "ps":
                    for q2, j in bank.get(k, {}).items():
                        dep(j, q2 != o["q"])
            for k in o["r"]:
                if k in last and k[:2] != "ps":
                    dep(last[k])
            for k in o["w"]:
                if k[:2] != "ps":
                    for j in ([last[k]] if k in last else []) + reads.get(k, []):
                        dep(j, ops[j]["q"] != o["q"] or k not in APART or ops[j]["fill"])
            for k in o["r"] + o["w"]:
                if k[:2] == "ps":
                    bank.setdefault(k, {})[o["q"]] = i
            for k in o["r"]:
                reads.setdefault(k, []).append(i)
            for k in o["w"]:
                if k in APART and k in last and ops[last[k]]["q"] == o["q"] and not reads.get(k):
                    dep(last[k], ops[last[k]]["fill"])
                last[k], reads[k] = i, []
        prio = [0.0] * n
        for i in range(n - 1, -1, -1):
            prio[i] += ops[i]["c"] + ops[i]["lat"]
            for j, full in pred[i].items():
                prio[j] = max(prio[j], prio[i] + (WAKE if full else 0.0))
        succ, left, ready = [[] for _ in ops], [len(p) for p in pred], [0.0] * n
        for i, p in enumerate(pred):
            for j, full in p.items():
                succ[j].append((i, full))
        free = {q: 0.0 for q in list(Q) + ["n"]}
        pool = {q: [] for q in free}
        for i in range(n):
            if not left[i]:
                pool[ops[i]["q"]].append(i)
        order = []
        while len(order) < n:
            best = min((max(free[q], min(ready[i] for i in pool[q])), q) for q in pool if pool[q])
            start, q = best
            i = max((x for x in pool[q] if ready[x] <= start + 1e-9), key=lambda x: prio[x])
            pool[q].remove(i)
            end = start + ops[i]["c"]
            free[q] = end if q != "n" else 0.0
            order.append(i)
            for j, full in succ[i]:
                ready[j] = max(ready[j], end + ops[i]["lat"] + WAKE if full else start)
                left[j] -= 1
                if not left[j]:
                    pool[ops[j]["q"]].append(j)
        return order

    def emit(q, f, r, w, dma, fill):
        own = "s" + q
        toks = []
        if q == "n":
            lw[w[0]] = [f]
            return
        for k in r + w:
            if k[:2] == "ps":
                toks += [x for x in acc.get(k, {}).values() if x[0] != own]
        for k in r:
            toks += lw.get(k, [])
        for k in w:
            toks += [x for x in lw.get(k, []) + rd.get(k, []) if x[0] != own or k not in APART] + filled.get(k, [])
        wait(q, toks)
        ins = f()
        if w and w[0][:3] == "snd":
            return
        if dma:
            s, n = "d%d" % ndma[0], 16
            ndma[0] += 1
        else:
            cnt[q] += 1
            s, n = own, cnt[q]
        ins.then_inc(T.sem[s], 16 if dma else 1)
        snap[(s, n)] = dict(know[q])
        tok = (s, n)
        for k in r + w:
            if k[:2] == "ps":
                acc.setdefault(k, {})[s] = tok
        for k in r:
            rd[k] = [x for x in rd.get(k, []) if x[0] != s] + [tok]
        for k in w:
            lw[k] = [tok]
            rd[k] = []
            if fill:
                filled[k] = [tok]

    vec, act = g.vector, g.scalar

    def v(name, a=0, b=None, p=None):
        ar, o, n = POS[name]
        b = n if b is None else b
        return T[ar][:, o + a:o + b] if p is None else T[ar][p[0]:p[1], o + a:o + b]

    def every(name, a, step):
        ar, o, n = POS[name]
        return T[ar][:, o + a:o + n:step]

    def V(f, r, w, n=0, k=1.0):
        n = n or SIZE.get(w.split()[0], 320)
        op("v", f, r, w, c=CYCLE * max(64.0, n * k))

    def cp(out, in_, r, w, n=0, k=1.0):
        if w in ON_ACT:
            ac(out, in_, r, w, n=n, k=k)
        else:
            V(lambda: vec.tensor_copy(out, in_), r, w, n, k)

    def ts(out, a, s1, s2, o1, o2, r, w, n=0):
        if w in ON_ACT:
            ac(out, a, r, w, n=n, scale=s1)
        elif o2 is None:
            V(lambda: vec.tensor_scalar(out, a, s1, None, o1), r, w, n)
        else:
            V(lambda: vec.tensor_scalar(out, a, s1, s2, o1, o2), r, w, n)

    def tt(out, a, b, o, r, w):
        V(lambda: vec.tensor_tensor(out, a, b, o), r, w, 0, 1.0 if r[:2] == "ps" else 2.0)

    def tr(out, in_, r, w):
        V(lambda: vec.transpose(out, in_), r, w)

    def scan(out, a, b, c, r, w):
        V(lambda: vec.tensor_tensor_scan(out, a, b, c, OP.add, OP.max), r, w)

    def red(out, in_, o, r, w, n=0):
        V(lambda: vec.tensor_reduce(out, in_, AxisListType.X, o), r, w, n)

    def fill(ap, c, w, n=0):
        op("v", lambda: vec.memset(ap, c), "", w, c=CYCLE * max(64.0, 0.5 * (n or SIZE.get(w, 320))), fill=True)

    def ac(out, in_, r, w, func=AF.Copy, n=0, k=1.0, fill=False, **kw):
        if w in ON_VEC:
            if "bias" in kw:
                ts(out, in_, kw["bias"], None, OP.add, None, r, w, n)
            elif "scale" in kw:
                ts(out, in_, kw["scale"], None, OP.mult, None, r, w, n)
            else:
                cp(out, in_, r, w, n, k)
            return
        op("a", lambda: act.activation(out, in_, func, **kw), r, w, c=CYCLE * max(64.0, k * (n or SIZE.get(w.split()[0], 320))) + (0.02 if "accum_out" in kw else 0.0), fill=fill)

    def quant(q, s, t_, r, w, n=320):
        op("v", lambda: vec.quantize_mx(q, s, t_), r, w, c=0.015 + 0.0011 * n)

    def mm(bank, n, L, M, r, start=True, stop=True):
        op("t", lambda: g.tensor.matmul_mx(T["ps%d" % bank][:, 0:n], L[0], L[1], M[0], M[1], start, stop), r, "ps%d" % bank, c=1.5 * CYCLE * (n + 16))

    def zeros(ap, n, w):
        ac(ap, v("zb", 0, n), "zb", w, n=n, fill=True)

    def iota(ap, pat, first, w, fl=False, cm=0, c=0.3, fill=False):
        op("g", lambda: g.iota(ap, pat, first, cm, **({"allow_small_or_imprecise_dtypes": True} if fl else {})), "", w, c=c, fill=fill)

    def load(dst, src, w):
        op("s", lambda: g.sync.dma_start(dst, src), "", w, dma=True, c=0.1)

    def store(dst, src, r):
        op("s", lambda: g.sync.dma_start(dst, src), r, "", dma=True, c=0.1)

    def ps(b, n=320):
        return T["ps%d" % b][:, 0:n]

    def pair(q, s, a, n):
        return (T[q][:, a:a + n], T[s][:, a:a + n])

    def kst(name):
        return pair("kq", "ks", 128 * KEYS.index(name), 128)

    def ust(name):
        return pair("upq", "ups", 128 * USEG.index(name), 128)

    def pcol(i):
        return v("pf", i, i + 1)
    Q16, P32, PAR, ME, MO, PG, PF, BE, BO, TBI, HSC, HOF = range(12)

    load(T.ut[:], T.u[:], "ut")
    load(T.xt[:], T.x[:], "xt")
    load(T.olt[:], T.ol[:], "olt")
    load(T.wq[:].bitcast(dt.uint8), T.wc[:], "wq")
    load(T.wsp[:], T.ws[:], "wsp")
    load(T.vt[:], T.v[:], "vt")
    for i, (pat, base) in enumerate([([[0, 8]], 8), ([[16, 8]], 0), ([[32, 4], [0, 2]], 0), ([[32, 4], [0, 2]], 16), ([[16, 8]], 1), ([[32, 4], [0, 2]], 1), ([[32, 4], [0, 2]], 17)]):
        iota(v("uli", 8 * i, 8 * i + 8), pat, base, "uli")
    iota(v("pii", 0, 1), [[0, 1]], 0, "p0", cm=1)
    iota(v("ci"), [[0, 20], [1, 16]], 0, "ci", True)
    iota(v("iof"), [[1, 320]], 0, "iof", True)
    iota(v("cg", 0, 128), [[2, 4], [0, 32]], 0, "cg", True)
    iota(v("cg", 128, 256), [[2, 4], [0, 32]], 1, "cg", True)
    iota(v("inm", 0, 6), [[-1, 6]], 6, "inm", True)
    iota(v("b16"), [[16, 20]], 0, "b16", True)
    iota(v("wqt"), [[0, 20], [-1, 6]], 6, "wqt", True)
    iota(v("eli"), [[1, 10], [0, 2]], 0, "eli")

    fill(v("zb"), 0.0, "zb")
    fill(v("rss"), 0.0, "rss")
    fill(v("rso"), 0.0, "rso")
    fill(v("own"), 0.0, "own0")
    cp(v("ul"), v("uli"), "uli", "ul")
    ts(v("pii", 1, 2), v("pii", 0, 1), 15, None, OP.bitwise_and, None, "p0", "p1")
    ts(v("pii", 2, 3), v("pii", 0, 1), 31, None, OP.bitwise_and, None, "p0", "p2")
    ts(v("pii", 4, 5), v("pii", 0, 1), 4, None, OP.logical_shift_right, None, "p0", "p4")
    ts(v("pii", 3, 4), v("pii", 4, 5), 1, None, OP.bitwise_and, None, "p4", "p3")
    for d, s in ((Q16, 1), (P32, 2), (PG, 4), (PF, 0), (PAR, 3)):
        cp(pcol(d), v("pii", s, s + 1), "p%d" % s, "pf%d" % d)
    ts(pcol(ME), pcol(PAR), -1.0, 1.0, OP.mult, OP.add, "pf2", "pf3")
    cp(pcol(MO), pcol(PAR), "pf2", "pf4")
    ts(pcol(BE), pcol(ME), BIG, None, OP.mult, None, "pf3", "pf7")
    ts(pcol(BO), pcol(MO), BIG, None, OP.mult, None, "pf4", "pf8")
    ts(v("ms"), v("ci"), pcol(Q16), pcol(BE), OP.is_ge, OP.mult, "ci pf0 pf7", "ms")
    quant(T.uq[:], T.us[:], T.ut[:], "ut", "uq")
    cp(T.upq[:].bitcast(dt.uint32), T.uq[:].bitcast(dt.uint32).indirect(v("ul")), "uq ul", "upq", 896, 1.6)
    ac(T.ups[:], T.us[:].indirect(v("ul")), "uq ul", "ups", n=896, k=1.6)
    quant(T.xq0[:], T.xs0[:], T.xt[:], "xt", "xq0c xq0s")
    ts(v("m1"), v("ci"), pcol(Q16), pcol(BO), OP.is_le, OP.mult, "ci pf0 pf8", "m1")
    tt(v("ms"), v("ms"), v("m1"), OP.add, "ms m1", "ms")
    zeros(T.TB[:], 1280, "TB")
    fill(T.eq[:], 0.0, "eq")
    for m in range(4, -1, -1):
        ac(T.TS[:, 1280 * m:1280 * m + 4 * NT[m]], v("zb", 0, 4 * NT[m]), "zb", "TS%d" % m, n=4 * NT[m], fill=True)

    def consts_births():
        fill(T.kt[:, 0:512], 512.0, "kt0")
        quant(*kst("KB"), T.kt[:, 0:512], "kt0", "kB")
        zeros(T.kt[:, 512:1536], 1024, "kt1")
        zeros(T.kt[:, 1536:2064], 528, "kt1")
        zeros(T.kt[:, 3088:3604], 516, "kt2")
        ts(T.kt[:, 3091:3603:4], v("iof", 0, 128), pcol(PF), 0.5, OP.is_equal, OP.mult, "iof pf6", "kt2")
        ts(T.kt[:, 515:1027:4], v("iof", 0, 128), pcol(PF), 128.0, OP.is_equal, OP.mult, "iof pf6", "kt1")
        for b in range(4):
            quant(*kst("KH%d" % b), T.kt[:, 3091 - b:3603 - b], "kt2", "kH%d" % b)
        ts(v("mo"), v("ms"), -1.0, None, OP.mult, None, "ms", "mo")

    def consts_order():
        for m in range(4, -1, -1):
            iota(T.TO[:, 1280 * m:1280 * m + 4 * NT[m]], [[0, 4 * NT[m]]], 0, "TO%d TP%d" % (m, m), True, c=0.13 + 8 * NT[m] * CYCLE, fill=True)
        ts(v("inm", 0, 6), v("inm", 0, 6), pcol(Q16), None, OP.is_equal, None, "inm pf0", "inm")
        ts(v("inm", 8, 14), v("inm", 0, 6), -1.0, None, OP.add, None, "inm", "inb")

    def consts_reading():
        for i, n in enumerate("eo"):
            m = v("gmk", 128 * i, 128 * i + 128)
            ts(m, v("cg", 128 * i, 128 * i + 128), pcol(PG), None, OP.is_equal, None, "cg pf5", "gm%d" % i)
            for b in range(4):
                cp(T.kt[:, 2064 + 512 * i + b:2064 + 512 * i + 512:4], m, "gm%d" % i, "kg%d" % i)
            o = 1028 + 516 * i
            for b in (2, 3):
                cp(T.kt[:, o + b:o + 512:4], m, "gm%d" % i, "kt1")
            quant(*kst("SD" + n), T.kt[:, o + 2:o + 514], "kt1", "kS" + n)
            quant(*kst("OD" + n), T.kt[:, o:o + 512], "kt1", "kO" + n)
            quant(*kst("G" + n), T.kt[:, 2064 + 512 * i:2576 + 512 * i], "kg%d" % i, "kG" + n)
        cp(v("lst0"), T.olt[:], "olt", "L0")
        ts(v("own"), v("own"), pcol(Q16), None, OP.add, None, "own0 pf0", "own0")
        tt(v("own"), v("b16"), v("own"), OP.add, "b16 own0", "own")
        ts(v("rsm"), v("wqt"), 6.0, None, OP.is_lt, None, "wqt", "rsm")
        ts(v("wqt"), v("wqt"), 262144.0, None, OP.mult, None, "wqt", "wqt")
        fill(v("yp"), 1.0, "yp")
        ts(v("bm"), v("ci"), pcol(Q16), None, OP.is_equal, None, "ci pf0", "bm")
        for o in (0, 1280, 2560):
            zeros(v("pk", o, min(o + 1280, 3200)), min(1280, 3200 - o), "pk")

    def consts_counts():
        ts(pcol(TBI), pcol(P32), -1.0, -0.5, OP.mult, OP.add, "pf1", "pf9")
        ts(pcol(HSC), pcol(MO), 1.0 / 4096 - 1.0, 1.0, OP.mult, OP.add, "pf4", "pf10")
        ts(pcol(HOF), pcol(MO), -0.3125, None, OP.mult, None, "pf4", "pf11")
        cp(v("el"), v("eli"), "eli", "el")
        fill(v("hc"), 0.0, "hc")
        fill(v("hw"), 0.0, "hw")
        fill(v("one"), 1.0, "one")
        quant(T.vq[:], T.vs[:], T.vt[:], "vt", "vq")
        for b in range(4):
            quant(*kst("KE%d" % b), T.kt[:, 515 - b:1027 - b], "kt1", "kE%d" % b)

    new_links = []

    def lists_of_links(t_):
        tr(T.lt[:], T.la[:], "la0 la1", "lt")
        ts(v("l1"), T.lt[:, :, 0], pcol(ME), None, OP.mult, None, "lt pf3", "l1")
        ts(v("l2"), T.lt[:, :, 16], pcol(MO), None, OP.mult, None, "lt pf4", "l2")
        tt(v("l3"), v("l1"), v("l2"), OP.add, "l1 l2", "l3")
        tt(v("li"), v("l3"), v("own"), OP.max, "l3 own", "li")
        ts(v("lj"), v("li"), 511, None, OP.bitwise_and, None, "li", "lj")
        cp(v("lst%d" % (t_ + 1)), v("lj"), "lj", "L%d" % (t_ + 1))

    for t in range(R):
        X = "xq%dc xq%ds" % (t, t)
        XA = pair("xq%d" % t, "xs%d" % t, 0, 320)
        L1, LK = v("lst%d" % t), "L%d" % t
        ux = "upq ups " + X

        for b, s in ((4, "USe"), (5, "USo"), (6, "US"), (0, "UB")):
            mm(b, 320, ust(s), XA, ux)
        for b, o in ((1, 0), (2, 128), (3, 192)):
            mm(b, 128, pair("xq%d" % t, "xs%d" % t, o, 128), ust("UB"), ux)
        mm(7, 320, ust("UO"), XA, ux)
        tt(T.alt[:, :, 0:16], ps(4), v("ms"), OP.add, "ps4 ms", "alt0")
        tt(T.alt[:, :, 16:32], ps(5), v("ms"), OP.add, "ps5 ms", "alt1")
        mm(4, 320, ust("UOe"), XA, ux)
        mm(5, 320, ust("UOo"), XA, ux)
        tr(T.lxs[:], T.alt[:], "alt0 alt1", "lxs")
        tt(v("sl"), T.lxs[:, :, 15], T.lxs[:, :, 16], OP.min, "lxs", "sl")
        ts(v("nsl"), v("sl"), -1.0, None, OP.mult, None, "sl", "nsl")
        tt(T.TD[:, 0:1280:4], ps(6), T.lxs[:, :, 0:16], OP.is_ge, "ps6 lxs", "TD0")
        tt(T.TD[:, 1:1280:4], ps(6), T.lxs[:, :, 16:32], OP.is_gt, "ps6 lxs", "TD1")

        def snapshots(ms_):
            for m in ms_:
                n, o, d = 16 * m, 1280 * (m // 4) + m % 4, "df%d" % (m % 4)
                ac(v(d, 0, n), ps(6, n), "ps6 nsl", d, AF.Relu, bias=v("nsl", m, m + 1), n=n)
                ac(T.TS[:, o:o + 4 * n:4], v(d, 0, n), d, "TS%d rss" % (m // 4), AF.Sign, accum_out=v("rss", m, m + 1), n=n)
        snapshots(range(19, EARLY - 1, -1))
        if new_links:
            lists_of_links(new_links.pop())
        for b in (0, 1):
            s, n = T["ps%d" % (b + 1)][:, 0:1], 128 * (b + 1)
            rr = "ps0 ps%d" % (b + 1)
            ts(T.eq[:, 128 * b:128 * b + 128], T.ps0[:, 128 * b:128 * b + 128], s, None, OP.is_equal, None, rr, "eq")
            ts(T.TB[:, b:4 * n:4], T.ps0[:, 0:n], s, None, OP.is_gt, None, rr, "TB")
            ts(T.TB[:, 4 * n + b:1280:4], T.ps0[:, n:320], s, None, OP.is_ge, None, rr, "TB")
        s = T.ps3[64:128, 0:1]
        ts(T.eq[64:128, 256:320], T.ps0[64:128, 256:320], s, None, OP.is_equal, None, "ps0 ps3", "eq")
        ts(T.TB[64:128, 2:1280:4], T.ps0[64:128, 0:320], s, None, OP.is_gt, None, "ps0 ps3", "TB")
        op("g", lambda: g.affine_select(T.TB[:, 3:1024:4], T.eq[:, 0:256], [[0, 2], [1, 128]], OP.is_gt, 0.0, 0, -1), "eq", "TBa")
        op("g", lambda: g.affine_select(T.TB[:, 1027:1280:4], T.eq[:, 256:320], [[1, 64]], OP.is_gt, 0.0, 64, -1), "eq", "TBb")
        if t == 0:
            consts_births()
        tt(T.alt[:, :, 0:16], ps(4), v("mo"), OP.add, "ps4 mo", "alt0")
        tt(T.alt[:, :, 16:32], ps(5), v("mo"), OP.add, "ps5 mo", "alt1")
        quant(T.bq[:], T.bs[:], T.TB[:], "TB TBa TBb", "bq")
        mm(0, 320, kst("KB"), (T.bq[:], T.bs[:]), "kB bq")
        for b in (1, 2, 3):
            mm(b, 320, kst("KH%d" % b), XA, "kH%d %s" % (b, X))
        tr(T.lxo[:], T.alt[:], "alt0 alt1", "lxo")
        tt(v("va"), ps(0), v("iof"), OP.add, "ps0 iof", "va")
        mm(0, 320, kst("KH0"), XA, "kH0 " + X)
        tt(v("slo"), T.lxo[:, :, 15], T.lxo[:, :, 16], OP.max, "lxo", "slo")
        tt(T.TD[:, 2:1280:4], ps(7), T.lxo[:, :, 0:16], OP.is_le, "ps7 lxo", "TD2")
        tt(T.TD[:, 3:1280:4], ps(7), T.lxo[:, :, 16:32], OP.is_lt, "ps7 lxo", "TD3")
        if t == 0:
            consts_order()
        for i in range(6):
            ac(v("inj", 320 * i, 320 * i + 320), v("va"), "va inm inb", "inj%d" % i, AF.Identity, bias=v("inm", 8 + i, 9 + i), scale=v("inm", i, i + 1))
        for b in (3, 1, 2, 0):
            ac(T.fw[:, 320 * b:320 * b + 320], ps(b), "ps%d" % b, "fw%d" % b)
        mm(5, 320, ust("UO"), XA, ux)
        snapshots(range(EARLY - 1, 0, -1))
        for m in range(19, 0, -1):
            if m not in ACT_ORDER:
                n, o = 16 * m, 1280 * (m // 4) + m % 4
                ts(T.TO[:, o:o + 4 * n:4], ps(7, n), v("slo", m, m + 1), None, OP.is_lt, None, "ps7 slo", "TO%d o%d" % (m // 4, m), n)
        if t == 0:
            consts_reading()
        quant(T.dq[:], T.ds[:], T.TD[:], "TD0 TD1 TD2 TD3", "dq")
        for m in range(19, 0, -1):
            n, o, d = 16 * m, 1280 * (m // 4) + m % 4, "df%d" % (m % 4)
            if m in ACT_ORDER:
                ac(v(d, 0, n), ps(5, n), "ps5 slo", d, AF.Relu, bias=v("slo", m, m + 1), scale=-1.0, n=n)
                ac(T.TO[:, o:o + 4 * n:4], v(d, 0, n), d, "TP%d rso" % (m // 4), AF.Sign, accum_out=v("rso", m, m + 1), n=n)
        for m in range(19, 0, -1):
            n, o = 16 * m, 1280 * (m // 4) + m % 4
            if m not in ACT_ORDER:
                d = "dump%d" % (m % 2)
                ac(v(d, 0, n), T.TO[:, o:o + 4 * n:4], "o%d" % m, d + " rso", AF.Copy, accum_out=v("rso", m, m + 1), n=n)
        if t == 0:
            consts_counts()
            for k in range(10):
                o = 352 * k
                ac(v("pk", o, o + 16), v("bm", 0, 16), "bm", "pk")
                ac(v("pk", o + 16, o + 32), v("bm", 0, 16), "bm", "pk", scale=4096.0)

        src, sk = v("inj", 0, 320), "inj0"
        for i in range(1, 6):
            d = "aw%d" % (i % 2)
            tt(v(d), src.indirect(L1), v("inj", 320 * i, 320 * i + 320), OP.max, "%s inj%d %s" % (sk, i, LK), d)
            src, sk = v(d), d
        ac(v("a6f"), src.indirect(L1), "%s %s" % (sk, LK), "a6f")
        ac(T.a6[:, :, 0:16], v("a6f"), "a6f", "a60")
        ac(T.a6[:, :, 16:32], v("a6f"), "a6f", "a61")

        def sums(tile, q, s, key, banks, pre):
            for i, n in enumerate("eo"):
                mm(banks[i], 320, kst(pre + n), (T.dq[:], T.ds[:]), "k%s%s dq" % (pre[0], n), True, False)
            for m in range(4, -1, -1):
                p = pair(q, s, 320 * m, NT[m])
                quant(p[0], p[1], T[tile][:, 1280 * m:1280 * m + 4 * NT[m]], key % ((m,) * key.count("%")), "q%s%d" % (tile, m), NT[m])
                for i, n in enumerate("eo"):
                    mm(banks[i], NT[m], kst("G" + n), p, "kG%s q%s%d" % (n, tile, m), False, m == 0)

        sums("TS", "sq", "ss", "TS%d", (4, 6), "SD")
        sums("TO", "oq", "osq", "TO%d TP%d", (5, 7), "OD")
        tt(v("plr"), v("b16"), v("rss"), OP.subtract, "b16 rss", "plr")
        ts(v("plq"), v("plr"), 512.0, 512.0, OP.mult, OP.add, "plr", "plq")
        tr(T.tt[:], T.a6[:], "a60 a61", "tt")
        ts(v("va6"), T.tt[:, :, 1:7], pcol(ME), None, OP.mult, None, "tt pf3", "va6")
        ts(v("vb6"), T.tt[:, :, 17:23], pcol(MO), None, OP.mult, None, "tt pf4", "vb6")
        tt(v("v6"), v("va6"), v("vb6"), OP.add, "va6 vb6", "v6")
        tt(v("vw"), v("v6"), v("wqt"), OP.add, "v6 wqt", "vw")
        cp(v("ti"), every("v6", 2, 6), "v6", "ti")
        ts(v("tj"), v("ti"), 511, None, OP.bitwise_and, None, "ti", "tj")
        cp(v("l3u"), v("tj"), "tj", "l3u")
        ac(T.cb[:, :, 0:16], ps(4), "ps4", "cb0", scale=512.0)
        ts(T.cb[:, :, 16:32], ps(6), 512.0, None, OP.mult, None, "ps6", "cb1")
        tr(T.cu[:], T.cb[:], "cb0 cb1", "cu")
        tt(v("pls"), v("plq"), T.cu[:, :, 0], OP.add, "plq cu", "pls")
        for i in range(5):
            tt(every("yp", i, 6), every("v6", i, 6), v("pls"), OP.is_lt, "v6 pls", "yp")
        tt(v("yq"), v("yp"), v("vw"), OP.mult, "yp vw", "yq")
        V(lambda: vec.tensor_tensor_scan(v("ys"), v("rsm"), v("yq"), 0.0, OP.mult, OP.max), "yq rsm", "ys")
        cp(v("ri"), every("ys", 5, 6), "ys", "ri")
        ts(v("rj"), v("ri"), 511, None, OP.bitwise_and, None, "ri", "rj")
        cp(v("rl"), v("rj"), "rj", "rl")
        for k in range(10 - VEC_COUNTS):
            if k == min(GATHER_AT, 9 - VEC_COUNTS):
                for b in range(4):
                    ac(v("zg%d" % b), T.fw[:, 320 * b:320 * b + 320].indirect(v("rl")), "fw%d rl" % b, "zg%d" % b)
            d = "hs%d" % (k % 2)
            ac(v(d), v("pk", 320 * k, 320 * k + 320).indirect(v("rl")), "pk rl", d + " hc", AF.Copy, accum_out=v("hc", k, k + 1))
        cp(T.ca[:, :, 0:16], ps(5), "ps5", "ca0")
        cp(T.ca[:, :, 16:32], ps(7), "ps7", "ca1")
        tr(T.ct[:], T.ca[:], "ca0 ca1", "ct")
        tt(v("plo"), v("b16"), v("rso"), OP.subtract, "b16 rso", "plo")
        tt(v("plo"), v("plo"), T.ct[:, :, 0], OP.add, "plo ct", "plo")
        cp(v("ru"), v("plo"), "plo", "ru")
        cp(v("er").indirect(v("ru")), v("iof"), "ru iof", "er", 320, 3.8)
        cp(T.ea[:, :, 0:16], v("er", 0, 128), "er", "ea0")
        cp(T.ea[:, :, 16:32], v("er", 0, 128), "er", "ea1")
        tr(T.et[:], T.ea[:], "ea0 ea1", "et")
        ts(v("e1"), T.et[:, :, 0], pcol(ME), None, OP.mult, None, "et pf3", "e1")
        ts(v("e2"), T.et[:, :, 16], pcol(MO), None, OP.mult, None, "et pf4", "e2")
        tt(v("ef"), v("e1"), v("e2"), OP.add, "e1 e2", "ef")
        for i in range(4):
            ts(v("e4", 8 * i, 8 * i + 8), v("ef"), 4.0, float(i), OP.mult, OP.add, "ef", "e4")
        cp(v("es%d" % t), v("ef"), "ef", "es%d" % t)
        for b in range(4):
            tt(T.zt[:, b:1280:4], ps(b), v("zg%d" % b), OP.add, "ps%d zg%d" % (b, b), "zt%d" % b)
        zk = "zt0 zt1 zt2 zt3"
        for b in range(4):
            cp(T.ett[:, b:512:4], T.zt[:].indirect(v("e4", 8 * b, 8 * b + 8)), zk + " e4", "ett%d" % b, 128, 2.0)
        HQ = pair("hq%d" % t, "hp%d" % t, 0, 128)
        quant(HQ[0], HQ[1], T.ett[:], "ett0 ett1 ett2 ett3", "hE%d" % t, 128)
        rid, pid = topo.addr(nxt)[0:2]
        eng = topo.engines(core, nxt)
        h = len(eng) // 2
        m1, m2 = sum(1 << e for e in eng[:h]), sum(1 << e for e in eng[h:])

        def send(dst, src_, sem, mask, key):
            rs = T.sem[sem + str(t)]
            op("g", lambda: g.remote_dma(dst, src_, rs, T.sem.rloc, pid, rid, mask), key, "snd" + sem + str(t), c=0.8)
        send(T["eland%d" % t][:], v("es%d" % t), "lA", m2, "es%d" % t)
        send(T["aq%d" % t][:].bitcast(dt.uint8), T["hq%d" % t][:].bitcast(dt.uint8), "cA", m1, "hE%d" % t)
        send(T["ap%d" % t][:], T["hp%d" % t][:], "pA", m2, "hE%d" % t)
        he = topo.engines(prv, core)
        for s, k, n in (("lA", "eland%d" % t, len(he) - len(he) // 2), ("cA", "aq%d" % t, len(he) // 2), ("pA", "ap%d" % t, len(he) - len(he) // 2)):
            op("n", (s + str(t), n), "snd" + s + str(t), k)
        zq, zs = T["zq%d" % t], T["zs%d" % t]
        quant(zq[:, 0:320], zs[:, 0:320], T.zt[:], zk, "zqa%d" % t)
        for k in range(10 - VEC_COUNTS, 10):
            cp(v("hv"), v("pk", 320 * k, 320 * k + 320).indirect(v("rl")), "pk rl", "hv")
            red(v("hc", k, k + 1), v("hv"), OP.add, "hv", "hd", 320)

        tr(v("h1"), v("hc"), "hc" + (" hd" if VEC_COUNTS else ""), "h1")
        for a in (0, 16):
            tt(v("h2", a, a + 16), v("h1", 0, 16), v("h1", 16, 32), OP.add, "h1", "h2")
        tt(v("h3", 0, 32, (0, 32)), v("h2", 0, 32, (0, 32)), v("h2", 0, 32, (32, 64)), OP.add, "h2", "h3a")
        tt(v("h3", 0, 32, (64, 96)), v("h2", 0, 32, (64, 96)), v("h2", 0, 32, (96, 128)), OP.add, "h2", "h3b")
        for a in range(4):
            tt(v("h4", 0, 32, (32 * a, 32 * a + 32)), v("h3", 0, 32, (0, 32)), v("h3", 0, 32, (64, 96)), OP.add, "h3a h3b", "h4")
        tr(v("h5"), v("h4"), "h4", "h5")
        ts(v("hi", 0, 10), v("h5", 0, 10), pcol(HSC), pcol(HOF), OP.mult, OP.add, "h5 pf10 pf11", "hi")
        ts(v("hj", 0, 10), v("hi", 0, 10), 4095, None, OP.bitwise_and, None, "hi", "hj")
        ts(v("hw", 0, 10), v("hj", 0, 10), 63.0, 1.0, OP.min, OP.add, "hj", "hw")
        ac(v("hx"), v("hw").indirect(v("el")), "hw el", "hx")
        tr(v("cf"), v("hx"), "hx", "cf")
        ac(v("dump0"), v("cf"), "cf pf9", "dump0 nv0", AF.Sign, bias=pcol(TBI), accum_out=v("nv", 0, 1))
        ts(v("nr", 0, 32), v("one"), v("nv", 0, 1), None, OP.mult, None, "one nv0", "nr0")
        tr(v("nr", 32, 64), v("nr", 0, 32), "nr0", "nr1")
        ts(v("nr", 64, 96), v("nr", 32, 64), 64.0, None, OP.is_gt, None, "nr1", "nr2")
        ts(v("nr", 96, 128), v("nr", 32, 64), 64.0, FAR, OP.is_le, OP.mult, "nr1", "nr3")
        red(v("nv", 1, 2), v("nr", 64, 96), OP.add, "nr2", "nv1")
        tt(v("nr", 128, 160), v("nr", 96, 128), v("nr", 32, 64), OP.add, "nr3 nr1", "nr4")
        red(v("nv", 2, 3), v("nr", 128, 160), OP.min, "nr4", "nv2")
        ts(v("ceq"), v("cf"), v("nv", 1, 2), 2.0, OP.is_equal, OP.mult, "cf nv1", "ceq")
        ts(v("nv", 3, 4), v("nv", 1, 2), 1024.0, None, OP.mult, None, "nv1", "nv3")
        tt(v("nv", 4, 5), v("nv", 3, 4), v("nv", 2, 3), OP.add, "nv3 nv2", "nv4")
        ac(v("ck"), v("cf"), "cf", "ck", scale=1024.0)
        scan(v("pe"), v("ceq"), v("zb", 0, 320), 64.0, "ceq zb", "pe")
        tt(v("py"), v("pe"), v("ck"), OP.add, "pe ck", "py")
        ts(v("gone"), v("py"), v("nv", 4, 5), None, OP.is_le, None, "py nv4", "gone")
        scan(v("pg"), v("gone"), v("zb", 0, 320), 319.0, "gone zb", "pg")
        ac(T.ga[:, :, 0:16], v("gone"), "gone", "ga0")
        ac(T.ga[:, :, 16:32], v("gone"), "gone", "ga1")
        ac(v("gn"), v("gone"), "gone", "gn", AF.Copy, scale=-FAR)
        cp(T.sa[:, :, 0:16], v("pg"), "pg", "sa0")
        ac(T.sa[:, :, 16:32], v("pg"), "pg", "sa1")
        tr(T.gt[:], T.ga[:], "ga0 ga1", "gt")
        tr(T.st[:], T.sa[:], "sa0 sa1", "st")
        tt(v("pq"), T.st[:, :, 0], T.gt[:, :, 0], OP.mult, "st gt", "pq")
        tt(v("sf"), v("pq"), v("own"), OP.max, "pq own", "sf")
        sel = v("sel%d" % t)
        cp(sel, v("sf"), "sf", "sel%d" % t)
        tt(v("kb0"), v("gn"), v("iof"), OP.add, "gn iof", "kb0")

        AQ = pair("aq%d" % t, "ap%d" % t, 0, 128)
        ak = "aq%d ap%d " % (t, t)
        for b in range(4):
            mm(4 + b, 128, pair("wq", "wsp", 128 * b, 128), AQ, "wq wsp " + ak, True, False)
            mm(4 + b, 128, kst("KE%d" % b), AQ, "kE%d %s" % (b, ak), False, True)
        for b in range(4):
            o = T.rt[:, b:512:4]
            if b % 2 == 0:
                ac(o, ps(4 + b, 128), "ps%d" % (4 + b), "rt%d" % b, scale=0.0078125)
            else:
                ts(o, ps(4 + b, 128), 0.0078125, None, OP.mult, None, "ps%d" % (4 + b), "rt%d" % b)
        quant(zq[:, 320:448], zs[:, 320:448], T.rt[:], "rt0 rt1 rt2 rt3", "zqb%d" % t)
        nx = "xq%d" % (t + 1)
        nq, ns = T[nx], T["xs%d" % (t + 1)]
        zz = "zqa%d zqb%d sel%d" % (t, t, t)
        cp(nq[:].bitcast(dt.uint32), zq[:].bitcast(dt.uint32).indirect(sel), zz, nx + "c", 320, 1.6)
        ac(ns[:], zs[:].indirect(sel), zz, nx + "s", n=320, k=1.6)
        if t == R - 1:
            nx = nx + "c " + nx + "s"
            mm(0, 320, (T.vq[:], T.vs[:]), (nq[:], ns[:]), "vq " + nx)
            store(T.oc[:], nq[:].bitcast(dt.uint8), nx)
            for k in range(4):
                store(T.osc[4 * k:4 * k + 4, :], ns[32 * k:32 * k + 4, :], nx)

        for i in range(1, 4):
            ac(v("kb%d" % i), v("kb0"), "kb0", "kb%d" % i, AF.Copy, bias=512.0 * i)
        tt(v("aw0"), v("kb1").indirect(L1), v("kb2"), OP.max, "kb1 kb2 " + LK, "aw0")
        tt(v("aw1"), v("aw0").indirect(L1), v("kb3"), OP.max, "aw0 kb3 " + LK, "aw1")
        ac(v("lw", 320, 448), v("iof").indirect(T["eland%d" % t][:]), "iof eland%d" % t, "lw1", AF.Copy, bias=512.0)
        ac(v("dw"), v("aw1").indirect(L1), "aw1 " + LK, "dw")
        ac(v("dx"), v("dw"), "dw", "dx", AF.Copy, bias=2048.0)
        tt(v("lw", 0, 320), v("dw").indirect(v("l3u")), v("dx"), OP.max, "dw dx l3u", "lw0")
        lsrc = v("lw").indirect(sel)
        if t == R - 1:
            ac(v("hs0"), ps(0), "ps0", "hs0")
            store(T.y[:], v("hs0"), "hs0")
            cp(v("lkf"), lsrc, "lw0 lw1 sel%d" % t, "lkf")
            tt(v("fi"), v("lkf"), v("iof"), OP.max, "lkf iof", "fi")
            ts(v("fj"), v("fi"), 511, None, OP.bitwise_and, None, "fi", "fj")
            cp(v("lkf"), v("fj"), "fj", "lkf")
            store(T.lk[:], T.fl[0:128:16, POS["lkf"][1]:POS["lkf"][1] + 320], "lkf")
        else:
            ac(v("lkf"), lsrc, "lw0 lw1 sel%d" % t, "lkf")
            ac(T.la[:, :, 0:16], v("lkf"), "lkf", "la0")
            ac(T.la[:, :, 16:32], v("lkf"), "lkf", "la1")
            new_links.append(t)
    for i in schedule():
        o = ops[i]
        emit(o["q"], o["f"], o["r"], o["w"], o["dma"], o["fill"])
    for q in ("v", "a", "t", "g"):
        g.wait_ge(T.sem["s" + q], cnt[q])
    for i in range(ndma[0]):
        g.wait_ge(T.sem["d%d" % i], 16)
    g.wait_ge(T.sem.rloc, R * (h + 2 * (len(eng) - h)))
